import numpy as np
import ml_dtypes


def mxq(x, axis, fmt="e4m3"):
    dtype, down = {"e4m3": (ml_dtypes.float8_e4m3fn, 7), "e5m2": (ml_dtypes.float8_e5m2, 14)}[fmt]
    v = np.moveaxis(np.asarray(x, np.float32).astype(ml_dtypes.bfloat16).astype(np.float64), axis, -1)
    blocks = v.reshape(v.shape[:-1] + (-1, 32))
    amax = np.abs(blocks).max(-1, keepdims=True)
    byte = np.maximum(np.where(amax > 0, np.frexp(amax)[1] - 1 + 127, 0) - down, 1)
    scale = np.exp2(byte - 127.0)
    codes = (blocks / scale).astype(np.float32).astype(dtype).astype(np.float64)
    return np.moveaxis((codes * scale).reshape(v.shape), -1, axis)


WIDE = False


def mx_kscale(k):
    if not WIDE:
        return np.ones(k)
    levels = np.array([10, -10, 5, -5, 0])
    if k % 512:
        return np.exp2(np.random.permutation(np.resize(levels, k // 32))).repeat(32)
    a = np.empty((k // 512, 16))
    for p in range(k // 512):
        a[p, :8] = np.random.permutation(np.resize(levels, 8))
        for g in range(8):
            far = levels[np.abs(levels - a[p, g]) >= 10]
            a[p, g + 8] = far[np.random.randint(len(far))]
    return np.exp2(a.ravel()).repeat(32)


BF16 = ml_dtypes.bfloat16


def bf(x):
    return np.asarray(x, np.float32).astype(BF16)


def f64(x):
    return np.asarray(x).astype(np.float64)


E2M1 = np.array([0.0, 0.5, 1.0, 1.5, 2.0, 3.0, 4.0, 6.0, -0.0, -0.5, -1.0, -1.5, -2.0, -3.0, -4.0, -6.0])


def pack_weight(w, fmt):
    k, n = w.shape
    w = f64(bf(w)).reshape(k // 32, 32, n)
    amax = np.abs(w).max(1)
    if fmt == "e4m3":
        byte = np.frexp(amax)[1] - 1 + 127 - 7
    else:
        mant, ex = np.frexp(amax / 6.0)
        byte = np.where(mant > 0.5, ex, ex - 1) + 127
    byte = np.clip(np.where(amax > 0, byte, 1), 1, 254)
    scaled = (w * np.exp2(127.0 - byte)[:, None, :]).reshape(k, n).astype(np.float32)
    by_word = np.ascontiguousarray(scaled.reshape(k // 512, 128, 4, n).transpose(0, 1, 3, 2))
    if fmt == "e4m3":
        words = by_word.astype(ml_dtypes.float8_e4m3fn).view(np.uint8)
    else:
        c = by_word.astype(ml_dtypes.float4_e2m1fn).view(np.uint8) & 0xF
        words = c[..., 0::2] | (c[..., 1::2] << 4)
    return np.ascontiguousarray(words), np.ascontiguousarray(byte.astype(np.uint8).reshape(k // 512, 16, n))


def unpack_weight(words, scales, fmt):
    g, p, n, _ = words.shape
    if fmt == "e4m3":
        vals = np.ascontiguousarray(words).view(ml_dtypes.float8_e4m3fn).astype(np.float64)
    else:
        nib = np.empty((g, p, n, 4), np.uint8)
        nib[..., 0::2] = words & 0xF
        nib[..., 1::2] = words >> 4
        vals = E2M1[nib]
    vals = vals * np.repeat(np.exp2(scales.astype(np.float64) - 127.0), 8, axis=1)[..., None]
    return vals.transpose(0, 1, 3, 2).reshape(g * 512, n)

def planes(Y):
    n, m = Y.shape
    b = f64(bf(Y)).reshape(n // 32, 32, m)
    amax = np.abs(b).max(1)
    byte = np.clip(np.where(amax > 0, np.frexp(amax)[1] - 1 + 127 - 7, 1), 1, 254)
    codes = (b * np.exp2(127.0 - byte)[:, None, :]).reshape(n, m).astype(np.float32).astype(ml_dtypes.float8_e4m3fn).view(np.uint8)
    words = codes.reshape(n // 512, 128, 4, m).transpose(0, 1, 3, 2)
    return np.ascontiguousarray(words), np.ascontiguousarray(byte.astype(np.uint8).reshape(n // 512, 16, m))


N, F, D, E = 1024, 1024, 1024, 1024


def sigmoid(z):
    return 1.0 / (1.0 + np.exp(-z))


def setup_inputs():
    s = mx_kscale(F)
    r = mx_kscale(N)
    t = np.random.standard_normal((N, F)) * s
    h = np.random.standard_normal((N, F)) * s
    v = np.random.standard_normal((F, D)) / np.sqrt(F) / s[:, None]
    v_words, v_scales = pack_weight(v, "e4m3")
    b = 0.3 * np.random.standard_normal(D)
    a = np.random.standard_normal((N, D))
    x = np.random.standard_normal((N, E)) / r[:, None]
    c = (1.0 + 0.1 * np.random.standard_normal(N)) * r
    return {"t": bf(t), "h": bf(h), "v_words": v_words, "v_scales": v_scales, "b": bf(b), "a": bf(a), "x": bf(x), "c": bf(c)}


def core(t, h, v_words, v_scales, b, a, x, c):
    n_rows = x.shape[0]
    vq = unpack_weight(v_words, v_scales, "e4m3")
    gt = np.tanh((mxq(f64(t), 1, "e4m3") @ vq) + f64(b)[None, :])
    gh = np.tanh((mxq(f64(h), 1, "e4m3") @ vq) + f64(b)[None, :])
    e = gt - gh
    q = f64(c)[:, None] * sigmoid(f64(a)) * e
    xq = mxq(f64(x), 0, "e4m3")
    u = (xq.T @ mxq(q, 0, "e4m3")) / np.sqrt(n_rows)
    return u


def reference(t, h, v_words, v_scales, b, a, x, c):
    R_out = core(t, h, v_words, v_scales, b, a, x, c)
    words, scales = planes(R_out.T)
    return R_out, words, scales

@@ -1,0 +1,396 @@
+from contextlib import ExitStack
+
+import concourse.mybir as mybir
+from concourse.masks import make_identity
+
+P = 128
+R = 1024
+FLOPS = 6 * R * R * R
+
+F32 = mybir.dt.float32
+BF16 = mybir.dt.bfloat16
+I32 = mybir.dt.int32
+U32 = mybir.dt.uint32
+U8 = mybir.dt.uint8
+X4 = mybir.dt.float8_e4m3fn_x4
+ACT = mybir.ActivationFunctionType
+ALU = mybir.AluOpType
+LT = 1
+LQ = 3
+LM = 1
+LS = 3
+LE = 1
+LEQ = 3
+LC = 1
+LX = 2
+LU = 1
+LUC = 2
+CENG = "V"
+
+
+def tile_differencetargetpropweightstep_x2_kernel(tc, t, h, v_words, v_scales, b, a, x, c, out_0, out_1, out_2):
+    nc = tc.nc
+    with ExitStack() as ctx:
+        keep = ctx.enter_context(tc.tile_pool(name="keep", bufs=1))
+        work = ctx.enter_context(tc.tile_pool(name="work", bufs=2))
+        psum = ctx.enter_context(tc.psum_pool(name="psum", bufs=8))
+
+        def bank():
+            return psum.tile([P, 512], F32, name="ps", tag="ps", bufs=8)
+
+        ctx.enter_context(tc.manual_schedule())
+        ident = keep.tile([P, P], F32, name="ident", align_bytes=64)
+        warm = keep.tile([P, 2], F32, name="warm")
+        v_codes = keep.tile([P, 2, R], U32, name="v_codes", align_bytes=64)
+        v_sc = keep.tile([P, 2, R], U8, name="v_sc", align_bytes=64)
+        b_rows = keep.tile([P, P], BF16, name="b_rows")
+        b_rows32 = keep.tile([P, P], F32, name="b_rows32", align_bytes=64)
+        b_col = keep.tile([P, 8], F32, name="b_col")
+        c_col = keep.tile([P, 2, 4], BF16, name="c_col")
+        x_codes = keep.tile([P, 2, R], U32, name="x_codes", align_bytes=64)
+        x_sc = keep.tile([P, 2, R], U8, name="x_sc", align_bytes=64)
+        q_codes = keep.tile([P, 2, R], U32, name="q_codes", align_bytes=64)
+        q_sc = keep.tile([P, 2, R], U8, name="q_sc", align_bytes=64)
+        o_codes = keep.tile([P, 2, R], U32, name="o_codes", align_bytes=64)
+        o_sc = keep.tile([P, 2, R], U8, name="o_sc", align_bytes=64)
+        codes = {}
+        scales = {}
+        for op in "th":
+            for g in range(2):
+                codes[op, g] = keep.tile([P, 2, 512], U32, name="codes_%s%d" % (op, g), align_bytes=64)
+                scales[op, g] = keep.tile([P, 2, 512], U8, name="scales_%s%d" % (op, g), align_bytes=64)
+        csig = [keep.tile([P, 4, R], F32, name="csig%d" % g, align_bytes=64) for g in range(2)]
+
+        nc.vector.memset(v_sc[:].rearrange("p g n -> p (g n)").bitcast(I32), 0)
+        nc.vector.memset(b_rows[:], 0.0)
+        nc.vector.memset(warm[:], 0.0)
+        make_identity(nc, ident[:])
+
+        src = {"t": t, "h": h, "x": x, "a": a}
+        raw = {}
+
+        def load(op, g, cuts=2):
+            r = work.tile([P, 4, R], BF16, name="raw", tag="raw", bufs=6, align_bytes=64)
+            raw[op, g] = r
+            view = src[op][512 * g : 512 * (g + 1), :].rearrange("(p j) f -> p j f", j=4)
+            w = 4 // cuts
+            for i in range(cuts):
+                nc.sync.dma_start(out=r[:, w * i : w * (i + 1), :], in_=view[:, w * i : w * (i + 1), :])
+
+        load("t", 0)
+        nc.scalar.dma_start(out=b_rows[0:8, :], in_=b.rearrange("(c p) -> c p", p=P))
+        for q in range(4):
+            nc.scalar.dma_start(
+                out=v_sc[32 * q : 32 * q + 4, :, :].bitcast(I32),
+                in_=v_scales[:, 4 * q : 4 * q + 4, :].rearrange("g q n -> q g n").bitcast(I32),
+            )
+        nc.scalar.dma_start(out=c_col[:], in_=c.rearrange("(g p j) -> p g j", g=2, j=4))
+        nc.scalar.activation(warm[:, 1:2], warm[:, 0:1], ACT.Sigmoid)
+        for g in range(2):
+            nc.sync.dma_start(
+                out=v_codes[:, g, :].bitcast(I32), in_=v_words[g].rearrange("p n t -> p (n t)").bitcast(I32)
+            )
+        load("x", 0)
+        load("h", 0)
+        load("x", 1)
+        load("a", 0)
+
+        def BIAS():
+            nc.vector.tensor_copy(out=b_rows32[:], in_=b_rows[:])
+            bp = bank()
+            nc.tensor.transpose(bp[:, 0:P], b_rows32[:], ident[:])
+            nc.vector.tensor_copy(out=b_col[:], in_=bp[:, 0:8])
+
+        pending = []
+
+        def later(n, key, fn):
+            pending.append([n, key, fn])
+
+        def tick():
+            due = []
+            for item in pending:
+                item[0] -= 1
+                if item[0] <= 0:
+                    due.append(item)
+            for item in due:
+                if item in pending:
+                    pending.remove(item)
+                    item[2]()
+
+        def need(key):
+            for item in list(pending):
+                if item[1] == key:
+                    pending.remove(item)
+                    item[2]()
+
+        def pcopy(eng, dst, srcv):
+            if eng == "V":
+                nc.vector.tensor_copy(out=dst, in_=srcv)
+            else:
+                nc.scalar.copy(out=dst, in_=srcv)
+
+        def T(op, g, jp, kg, eng):
+            ps = bank()
+            for jj in range(2):
+                words = raw[op, g][:, 2 * jp + jj, 512 * kg : 512 * (kg + 1)].bitcast(F32)
+                for u in range(2):
+                    o = 256 * jj + 128 * u
+                    nc.tensor.transpose(ps[:, o : o + 128], words[:, u:256:2], ident[:])
+            gr = work.tile([P, 256, 4], BF16, name="gr", tag="gr", bufs=6, align_bytes=64)
+            cols = slice(256 * jp, 256 * (jp + 1))
+
+            def evac():
+                dst = gr[:].bitcast(F32).rearrange("p (j n) u -> p j n u", j=2)
+                pcopy(eng, dst, ps[:].rearrange("p (j u n) -> p j n u", j=2, u=2))
+
+            def quant():
+                nc.vector.quantize_mx(
+                    out=codes[op, g][:, kg, cols].bitcast(X4),
+                    scales=scales[op, g][:, kg, cols],
+                    in_=gr[:].rearrange("p n k -> p (n k)"),
+                )
+
+            later(LT, ("c", op, g), evac)
+            later(LQ, ("c", op, g), quant)
+            tick()
+
+        tanhs = {}
+        es = {}
+
+        def M(op, g, dt):
+            need(("c", op, g))
+            ps = bank()
+            for kg in range(2):
+                nc.tensor.matmul_mx(
+                    out=ps[:],
+                    lhsT=v_codes[:, kg, P * dt : P * (dt + 1)].bitcast(X4),
+                    lhsT_scale=v_sc[:, kg, P * dt : P * (dt + 1)],
+                    rhs=codes[op, g][:, kg, :].bitcast(X4),
+                    rhs_scale=scales[op, g][:, kg, :],
+                    start=(kg == 0),
+                    stop=(kg == 1),
+                )
+
+            def tanh():
+                th = work.tile([P, 512], F32, name="th_" + op, tag="th_" + op, bufs=(9 if op == "t" else 3), align_bytes=64)
+                nc.scalar.activation(th[:], ps[:], ACT.Tanh, bias=b_col[:, dt : dt + 1])
+                tanhs[op, g, dt] = th
+
+            def sub():
+                e = work.tile([P, 512], F32, name="e", tag="e", bufs=5, align_bytes=64)
+                nc.vector.tensor_tensor(out=e[:], in0=tanhs["t", g, dt][:], in1=tanhs["h", g, dt][:], op=ALU.subtract)
+                es[g, dt] = e
+
+            later(LM, ("e", g, dt), tanh)
+            if op == "h":
+                later(LS, ("e", g, dt), sub)
+            tick()
+
+        qb = {}
+
+        def E(g, dt):
+            need(("e", g, dt))
+            ps = bank()
+            e = es[g, dt]
+            for j in range(4):
+                nc.tensor.transpose(ps[:, P * j : P * (j + 1)], e[:, P * j : P * (j + 1)], ident[:])
+
+            def mul():
+                need(("s", g, dt // 2))
+                if dt % 4 == 0:
+                    qb[g, dt // 4] = work.tile([P, 512, 4], BF16, name="qb", tag="qb", bufs=2, align_bytes=64)
+                nc.vector.tensor_tensor(
+                    out=qb[g, dt // 4][:, P * (dt % 4) : P * (dt % 4 + 1), :],
+                    in0=ps[:].rearrange("p (j d) -> p d j", j=4),
+                    in1=csig[g][:, :, P * dt : P * (dt + 1)].rearrange("p j d -> p d j"),
+                    op=ALU.mult,
+                )
+
+            def quant():
+                cols = slice(512 * (dt // 4), 512 * (dt // 4 + 1))
+                nc.vector.quantize_mx(
+                    out=q_codes[:, g, cols].bitcast(X4),
+                    scales=q_sc[:, g, cols],
+                    in_=qb[g, dt // 4][:].rearrange("p d j -> p (d j)"),
+                )
+
+            later(LE, ("q", g, dt // 4), mul)
+            if dt % 4 == 3:
+                later(LEQ, ("q", g, dt // 4), quant)
+            tick()
+
+        def SIG(g, k):
+            cols = slice(256 * k, 256 * (k + 1))
+            nc.scalar.activation(csig[g][:, :, cols], raw["a", g][:, :, cols], ACT.Sigmoid)
+
+            def cmul():
+                for j in range(4):
+                    s = csig[g][:, j, cols]
+                    if CENG == "V":
+                        nc.vector.tensor_scalar(out=s, in0=s, scalar1=c_col[:, g, j : j + 1], scalar2=None, op0=ALU.mult)
+                    else:
+                        nc.gpsimd.tensor_scalar(
+                            out=s, in0=s, scalar1=c_col[:, g, j : j + 1], scalar2=0.0, op0=ALU.mult, op1=ALU.add
+                        )
+
+            later(LC, ("s", g, k), cmul)
+
+        def X(g, half, XENG="V"):
+            xg = work.tile([P, 512, 4], BF16, name="xg", tag="xg", bufs=2, align_bytes=64)
+            cols = slice(512 * half, 512 * (half + 1))
+            if XENG == "V":
+                nc.vector.tensor_copy(out=xg[:], in_=raw["x", g][:, :, cols].rearrange("p j e -> p e j"))
+            elif XENG == "A":
+                nc.scalar.copy(out=xg[:], in_=raw["x", g][:, :, cols].rearrange("p j e -> p e j"))
+            else:
+                for i in range(4):
+                    cc = slice(512 * half + 128 * i, 512 * half + 128 * (i + 1))
+                    nc.gpsimd.tensor_scalar(
+                        out=xg[:, 128 * i : 128 * (i + 1), :],
+                        in0=raw["x", g][:, :, cc].rearrange("p j e -> p e j"),
+                        scalar1=1.0, scalar2=0.0, op0=ALU.mult, op1=ALU.add,
+                    )
+
+            def quant():
+                nc.vector.quantize_mx(
+                    out=x_codes[:, g, cols].bitcast(X4), scales=x_sc[:, g, cols], in_=xg[:].rearrange("p e j -> p (e j)")
+                )
+
+            later(LX, ("x", g), quant)
+
+        ub = {}
+
+        def S2(G, et, eng):
+            for g in range(2):
+                need(("x", g))
+                need(("q", g, G))
+            ps = bank()
+            for g in range(2):
+                nc.tensor.matmul_mx(
+                    out=ps[:],
+                    lhsT=x_codes[:, g, P * et : P * (et + 1)].bitcast(X4),
+                    lhsT_scale=x_sc[:, g, P * et : P * (et + 1)],
+                    rhs=q_codes[:, g, 512 * G : 512 * (G + 1)].bitcast(X4),
+                    rhs_scale=q_sc[:, g, 512 * G : 512 * (G + 1)],
+                    start=(g == 0),
+                    stop=(g == 1),
+                )
+            uf = work.tile([P, 512], F32, name="uf", tag="uf", bufs=8, align_bytes=64)
+            u16 = work.tile([P, 512], BF16, name="u16", tag="u16", bufs=8, align_bytes=64)
+            ub[G, et] = u16
+
+            def evac():
+                if eng == "A":
+                    nc.scalar.activation(uf[:], ps[:], ACT.Copy, scale=1.0 / 32.0)
+                else:
+                    nc.vector.tensor_scalar(out=uf[:], in0=ps[:], scalar1=1.0 / 32.0, scalar2=None, op0=ALU.mult)
+                nc.sync.dma_start(out=out_0[P * et : P * (et + 1), 512 * G : 512 * (G + 1)], in_=uf[:])
+
+            def cast():
+                nc.vector.tensor_copy(
+                    out=u16[:].rearrange("e (u w i) -> e u w i", u=2, i=2),
+                    in_=uf[:].rearrange("e (w u i) -> e u w i", u=2, i=2),
+                )
+
+            later(LU, ("u", G, et), evac)
+            later(LUC, ("u", G, et), cast)
+            tick()
+
+        def U(G, ep, eng):
+            need(("u", G, 2 * ep))
+            need(("u", G, 2 * ep + 1))
+            ps = bank()
+            for i in range(2):
+                words = ub[G, 2 * ep + i][:].bitcast(F32)
+                for u in range(2):
+                    o = 256 * i + 128 * u
+                    nc.tensor.transpose(ps[:, o : o + 128], words[:, 128 * u : 128 * (u + 1)], ident[:])
+            pg = work.tile([P, 256, 4], BF16, name="pg", tag="pg", bufs=3, align_bytes=64)
+            cols = slice(256 * ep, 256 * (ep + 1))
+
+            def evac():
+                dst = pg[:].bitcast(F32).rearrange("p (i e) u -> p i e u", i=2)
+                pcopy(eng, dst, ps[:].rearrange("p (i u e) -> p i e u", i=2, u=2))
+
+            def quant():
+                nc.vector.quantize_mx(
+                    out=o_codes[:, G, cols].bitcast(X4), scales=o_sc[:, G, cols], in_=pg[:].rearrange("p e j -> p (e j)")
+                )
+                if ep % 2:
+                    cc = slice(512 * (ep // 2), 512 * (ep // 2 + 1))
+                    nc.sync.dma_start(
+                        out=out_1[G, :, cc, :].rearrange("p m t -> p (m t)").bitcast(I32),
+                        in_=o_codes[:, G, cc].bitcast(I32),
+                    )
+                if ep == 3:
+                    for q in range(4):
+                        nc.sync.dma_start(
+                            out=out_2[G, 4 * q : 4 * q + 4, :].bitcast(I32),
+                            in_=o_sc[32 * q : 32 * q + 4, G, :].bitcast(I32),
+                        )
+
+            later(LT, ("o", G, ep), evac)
+            later(LQ, ("o", G, ep), quant)
+            tick()
+
+        BANKS = [(0, 0), (0, 1), (1, 0), (1, 1)]
+        for i, (jp, kg) in enumerate(BANKS):
+            T("t", 0, jp, kg, "VA"[i % 2])
+        load("t", 1)
+        BIAS()
+        for dt in range(8):
+            M("t", 0, dt)
+            if dt == 3:
+                X(0, 0)
+            if dt == 6:
+                X(0, 1)
+        load("h", 1)
+        for i, (jp, kg) in enumerate(BANKS):
+            T("h", 0, jp, kg, "VA"[i % 2])
+        load("a", 1)
+        tiles = [("t", 1, jp, kg) for jp, kg in BANKS] + [("h", 1, jp, kg) for jp, kg in BANKS]
+        for dt in range(0, 8, 2):
+            SIG(0, dt // 2)
+            M("h", 0, dt)
+            M("h", 0, dt + 1)
+            if dt == 0:
+                X(1, 0)
+            if dt == 2:
+                X(1, 1)
+            T(*tiles[dt], "A")
+            T(*tiles[dt + 1], "A")
+            if dt >= 2:
+                E(0, dt - 2)
+                E(0, dt - 1)
+        for dt in range(0, 8, 2):
+            SIG(1, dt // 2)
+            for i in range(2):
+                M("t", 1, dt + i)
+                M("h", 1, dt + i)
+            if dt == 0:
+                E(0, 6)
+                E(0, 7)
+            else:
+                E(1, dt - 2)
+                E(1, dt - 1)
+        for et in range(4):
+            S2(0, et, "A")
+        E(1, 6)
+        E(1, 7)
+        for et in range(4, 8):
+            S2(0, et, "A")
+        U(0, 0, "V")
+        U(0, 1, "V")
+        for et in range(4):
+            S2(1, et, "A")
+        U(0, 2, "V")
+        U(0, 3, "V")
+        for et in range(4, 8):
+            S2(1, et, "AV"[et % 2])
+        U(1, 0, "A")
+        U(1, 1, "V")
+        tick()
+        U(1, 2, "A")
+        U(1, 3, "V")
+        for i in range(8):
+            tick()

@@ -16,16 +16,130 @@ X4 = mybir.dt.float8_e4m3fn_x4
 ACT = mybir.ActivationFunctionType
 ALU = mybir.AluOpType
 LT = 1
-LQ = 3
+LQ = 4
 LM = 1
-LS = 3
-LE = 1
-LEQ = 3
-LC = 1
-LX = 2
-LU = 1
-LUC = 2
+LS = 6
+LE = 3
+LEQ = 5
+LC = 7
+LX = 3
+LU = 2
+LUC = 5
 CENG = "V"
+ACCS = [[0,2],[0,4],[0,6],[1,4],[1,6],[1,2],[0,1]]
+PROG = [
+    ["load","t",0],
+    ["loadv"],
+    ["load","x",0,0],
+    ["load","x",0,1],
+    ["T","t",0,0,1,"V"],
+    ["load","h",0],
+    ["T","t",0,0,0,"A"],
+    ["load","x",1],
+    ["T","t",0,1,0,"A"],
+    ["load","a",0],
+    ["BIAS"],
+    ["T","t",0,1,1,"A"],
+    ["load","t",1],
+    ["M","t",0,3],
+    ["M","t",0,1],
+    ["load","h",1],
+    ["X",0,0,"V"],
+    ["X",0,1,"V"],
+    ["M","t",0,4],
+    ["M","t",0,2],
+    ["M","t",0,5],
+    ["M","t",0,7],
+    ["X",1,0,"V"],
+    ["T","h",0,0,1,"V"],
+    ["M","t",0,0],
+    ["T","h",0,0,0,"A"],
+    ["T","h",0,1,0,"A"],
+    ["SIG",0,0],
+    ["load","a",1],
+    ["T","h",0,1,1,"V"],
+    ["M","t",0,6],
+    ["M","h",0,0],
+    ["M","h",0,2],
+    ["X",1,1,"V"],
+    ["T","t",1,0,0,"A"],
+    ["T","t",1,1,0,"A"],
+    ["T","t",1,0,1,"V"],
+    ["M","h",0,1],
+    ["M","h",0,5],
+    ["M","h",0,3],
+    ["SIG",0,1],
+    ["T","t",1,1,1,"V"],
+    ["T","h",1,0,1,"V"],
+    ["E",0,0],
+    ["M","h",0,4],
+    ["E",0,1],
+    ["T","h",1,0,0,"A"],
+    ["M","t",1,5],
+    ["T","h",1,1,0,"A"],
+    ["T","h",1,1,1,"A"],
+    ["M","t",1,0],
+    ["M","h",0,7],
+    ["E",0,4],
+    ["E",0,5],
+    ["SIG",1,0],
+    ["M","t",1,1],
+    ["M","h",1,0],
+    ["E",0,2],
+    ["E",0,3],
+    ["M","t",1,2],
+    ["M","h",0,6],
+    ["M","t",1,3],
+    ["M","h",1,1],
+    ["M","h",1,3],
+    ["E",0,7],
+    ["E",0,6],
+    ["E",1,0],
+    ["M","h",1,2],
+    ["M","h",1,5],
+    ["M","t",1,4],
+    ["M","h",1,4],
+    ["E",1,2],
+    ["E",1,3],
+    ["E",1,1],
+    ["SIG",1,1],
+    ["M","t",1,6],
+    ["M","t",1,7],
+    ["M","h",1,7],
+    ["M","h",1,6],
+    ["E",1,4],
+    ["E",1,5],
+    ["S2",0,0,"A"],
+    ["S2",0,1,"A"],
+    ["S2",0,2,"A"],
+    ["S2",0,3,"A"],
+    ["S2",0,6,"A"],
+    ["E",1,6],
+    ["E",1,7],
+    ["S2",0,7,"A"],
+    ["S2",0,4,"A"],
+    ["S2",0,5,"A"],
+    ["U",0,0,"A"],
+    ["U",0,1,"V"],
+    ["S2",1,6,"A"],
+    ["S2",1,2,"A"],
+    ["S2",1,3,"A"],
+    ["S2",1,0,"A"],
+    ["U",0,2,"V"],
+    ["U",0,3,"A"],
+    ["S2",1,1,"A"],
+    ["S2",1,4,"A"],
+    ["S2",1,5,"A"],
+    ["S2",1,7,"A"],
+    ["U",1,0,"A"],
+    ["U",1,1,"A"],
+    ["U",1,2,"A"],
+    ["U",1,3,"A"],
+]
+
+
+def ACC(g, dt):
+    return [g, dt] in ACCS
 
 
 def tile_differencetargetpropweightstep_x2_kernel(tc, t, h, v_words, v_scales, b, a, x, c, out_0, out_1, out_2):
@@ -69,15 +183,17 @@ def tile_differencetargetpropweightstep_x2_kernel(tc, t, h, v_words, v_scales, b
         src = {"t": t, "h": h, "x": x, "a": a}
         raw = {}
 
-        def load(op, g, cuts=2):
-            r = work.tile([P, 4, R], BF16, name="raw", tag="raw", bufs=6, align_bytes=64)
-            raw[op, g] = r
+        def load(op, g, part=None):
+            if (op, g) not in raw:
+                raw[op, g] = work.tile([P, 4, R], BF16, name="raw", tag="raw", bufs=6, align_bytes=64)
             view = src[op][512 * g : 512 * (g + 1), :].rearrange("(p j) f -> p j f", j=4)
-            w = 4 // cuts
-            for i in range(cuts):
-                nc.sync.dma_start(out=r[:, w * i : w * (i + 1), :], in_=view[:, w * i : w * (i + 1), :])
+            for i in range(2) if part is None else [part]:
+                if op == "x":
+                    cols = slice(512 * i, 512 * (i + 1))
+                    nc.sync.dma_start(out=raw[op, g][:, :, cols], in_=view[:, :, cols])
+                else:
+                    nc.sync.dma_start(out=raw[op, g][:, 2 * i : 2 * i + 2, :], in_=view[:, 2 * i : 2 * i + 2, :])
 
-        load("t", 0)
         nc.scalar.dma_start(out=b_rows[0:8, :], in_=b.rearrange("(c p) -> c p", p=P))
         for q in range(4):
             nc.scalar.dma_start(
@@ -86,20 +202,21 @@ def tile_differencetargetpropweightstep_x2_kernel(tc, t, h, v_words, v_scales, b
             )
         nc.scalar.dma_start(out=c_col[:], in_=c.rearrange("(g p j) -> p g j", g=2, j=4))
         nc.scalar.activation(warm[:, 1:2], warm[:, 0:1], ACT.Sigmoid)
-        for g in range(2):
-            nc.sync.dma_start(
-                out=v_codes[:, g, :].bitcast(I32), in_=v_words[g].rearrange("p n t -> p (n t)").bitcast(I32)
-            )
-        load("x", 0)
-        load("h", 0)
-        load("x", 1)
-        load("a", 0)
+        def loadv():
+            for g in range(2):
+                nc.sync.dma_start(
+                    out=v_codes[:, g, :].bitcast(I32), in_=v_words[g].rearrange("p n t -> p (n t)").bitcast(I32)
+                )
+
+
+        nb_col = keep.tile([P, 8], F32, name="nb_col")
 
         def BIAS():
             nc.vector.tensor_copy(out=b_rows32[:], in_=b_rows[:])
             bp = bank()
             nc.tensor.transpose(bp[:, 0:P], b_rows32[:], ident[:])
             nc.vector.tensor_copy(out=b_col[:], in_=bp[:, 0:8])
+            nc.vector.tensor_scalar(out=nb_col[:], in0=b_col[:], scalar1=-1.0, scalar2=None, op0=ALU.mult)
 
         pending = []
 
@@ -123,6 +240,8 @@ def tile_differencetargetpropweightstep_x2_kernel(tc, t, h, v_words, v_scales, b
                     pending.remove(item)
                     item[2]()
 
+        grouped = {}
+
         def pcopy(eng, dst, srcv):
             if eng == "V":
                 nc.vector.tensor_copy(out=dst, in_=srcv)
@@ -136,22 +255,24 @@ def tile_differencetargetpropweightstep_x2_kernel(tc, t, h, v_words, v_scales, b
                 for u in range(2):
                     o = 256 * jj + 128 * u
                     nc.tensor.transpose(ps[:, o : o + 128], words[:, u:256:2], ident[:])
-            gr = work.tile([P, 256, 4], BF16, name="gr", tag="gr", bufs=6, align_bytes=64)
-            cols = slice(256 * jp, 256 * (jp + 1))
+            if jp == 0:
+                grouped[op, g, kg] = work.tile([P, 512, 4], BF16, name="gr", tag="gr", bufs=4, align_bytes=64)
+            gr = grouped[op, g, kg]
 
             def evac():
-                dst = gr[:].bitcast(F32).rearrange("p (j n) u -> p j n u", j=2)
+                dst = gr[:, 256 * jp : 256 * (jp + 1), :].bitcast(F32).rearrange("p (j n) u -> p j n u", j=2)
                 pcopy(eng, dst, ps[:].rearrange("p (j u n) -> p j n u", j=2, u=2))
 
             def quant():
                 nc.vector.quantize_mx(
-                    out=codes[op, g][:, kg, cols].bitcast(X4),
-                    scales=scales[op, g][:, kg, cols],
+                    out=codes[op, g][:, kg, :].bitcast(X4),
+                    scales=scales[op, g][:, kg, :],
                     in_=gr[:].rearrange("p n k -> p (n k)"),
                 )
 
             later(LT, ("c", op, g), evac)
-            later(LQ, ("c", op, g), quant)
+            if jp == 1:
+                later(LQ, ("c", op, g), quant)
             tick()
 
         tanhs = {}
@@ -172,17 +293,20 @@ def tile_differencetargetpropweightstep_x2_kernel(tc, t, h, v_words, v_scales, b
                 )
 
             def tanh():
-                th = work.tile([P, 512], F32, name="th_" + op, tag="th_" + op, bufs=(9 if op == "t" else 3), align_bytes=64)
-                nc.scalar.activation(th[:], ps[:], ACT.Tanh, bias=b_col[:, dt : dt + 1])
+                th = work.tile([P, 512], F32, name="th_" + op, tag="th_" + op, bufs=(9 if op == "t" else 4), align_bytes=64)
+                if op == "h" and ACC(g, dt):
+                    nc.scalar.activation(th[:], ps[:], ACT.Tanh, bias=nb_col[:, dt : dt + 1], scale=-1.0)
+                else:
+                    nc.scalar.activation(th[:], ps[:], ACT.Tanh, bias=b_col[:, dt : dt + 1])
                 tanhs[op, g, dt] = th
 
             def sub():
-                e = work.tile([P, 512], F32, name="e", tag="e", bufs=5, align_bytes=64)
+                e = work.tile([P, 512], F32, name="e", tag="e", bufs=3, align_bytes=64)
                 nc.vector.tensor_tensor(out=e[:], in0=tanhs["t", g, dt][:], in1=tanhs["h", g, dt][:], op=ALU.subtract)
                 es[g, dt] = e
 
             later(LM, ("e", g, dt), tanh)
-            if op == "h":
+            if op == "h" and not ACC(g, dt):
                 later(LS, ("e", g, dt), sub)
             tick()
 
@@ -191,12 +315,18 @@ def tile_differencetargetpropweightstep_x2_kernel(tc, t, h, v_words, v_scales, b
         def E(g, dt):
             need(("e", g, dt))
             ps = bank()
-            e = es[g, dt]
             for j in range(4):
-                nc.tensor.transpose(ps[:, P * j : P * (j + 1)], e[:, P * j : P * (j + 1)], ident[:])
+                js = slice(P * j, P * (j + 1))
+                if ACC(g, dt):
+                    for op in "th":
+                        nc.tensor.matmul(
+                            ps[:, js], tanhs[op, g, dt][:, js], ident[:], start=(op == "t"), stop=(op == "h"), is_transpose=True
+                        )
+                else:
+                    nc.tensor.transpose(ps[:, js], es[g, dt][:, js], ident[:])
 
             def mul():
-                need(("s", g, dt // 2))
+                need(("s", g, dt // 4))
                 if dt % 4 == 0:
                     qb[g, dt // 4] = work.tile([P, 512, 4], BF16, name="qb", tag="qb", bufs=2, align_bytes=64)
                 nc.vector.tensor_tensor(
@@ -220,7 +350,7 @@ def tile_differencetargetpropweightstep_x2_kernel(tc, t, h, v_words, v_scales, b
             tick()
 
         def SIG(g, k):
-            cols = slice(256 * k, 256 * (k + 1))
+            cols = slice(512 * k, 512 * (k + 1))
             nc.scalar.activation(csig[g][:, :, cols], raw["a", g][:, :, cols], ACT.Sigmoid)
 
             def cmul():
@@ -259,6 +389,8 @@ def tile_differencetargetpropweightstep_x2_kernel(tc, t, h, v_words, v_scales, b
             later(LX, ("x", g), quant)
 
         ub = {}
+        ufs = {}
+        pgs = {}
 
         def S2(G, et, eng):
             for g in range(2):
@@ -275,46 +407,58 @@ def tile_differencetargetpropweightstep_x2_kernel(tc, t, h, v_words, v_scales, b
                     start=(g == 0),
                     stop=(g == 1),
                 )
-            uf = work.tile([P, 512], F32, name="uf", tag="uf", bufs=8, align_bytes=64)
-            u16 = work.tile([P, 512], BF16, name="u16", tag="u16", bufs=8, align_bytes=64)
-            ub[G, et] = u16
+            if et % 2 == 0:
+                ufs[G, et // 2] = work.tile([P, 2, 512], F32, name="uf", tag="uf", bufs=4, align_bytes=64)
+                ub[G, et // 2] = work.tile([P, 1024], BF16, name="u16", tag="u16", bufs=3, align_bytes=64)
+            uf = ufs[G, et // 2]
+            u16 = ub[G, et // 2]
+            i = et % 2
 
             def evac():
                 if eng == "A":
-                    nc.scalar.activation(uf[:], ps[:], ACT.Copy, scale=1.0 / 32.0)
+                    nc.scalar.activation(uf[:, i, :], ps[:], ACT.Copy, scale=1.0 / 32.0)
                 else:
-                    nc.vector.tensor_scalar(out=uf[:], in0=ps[:], scalar1=1.0 / 32.0, scalar2=None, op0=ALU.mult)
-                nc.sync.dma_start(out=out_0[P * et : P * (et + 1), 512 * G : 512 * (G + 1)], in_=uf[:])
+                    nc.vector.tensor_scalar(out=uf[:, i, :], in0=ps[:], scalar1=1.0 / 32.0, scalar2=None, op0=ALU.mult)
 
             def cast():
                 nc.vector.tensor_copy(
                     out=u16[:].rearrange("e (u w i) -> e u w i", u=2, i=2),
-                    in_=uf[:].rearrange("e (w u i) -> e u w i", u=2, i=2),
+                    in_=uf[:].rearrange("e k (w u i) -> e u (k w) i", u=2, i=2),
+                )
+                nc.sync.dma_start(
+                    out=out_0[P * (et - 1) : P * (et + 1), 512 * G : 512 * (G + 1)].rearrange("(k e) d -> e k d", k=2),
+                    in_=uf[:],
                 )
 
-            later(LU, ("u", G, et), evac)
-            later(LUC, ("u", G, et), cast)
+            later(LU, ("u", G, et // 2), evac)
+            if i:
+                later(LUC, ("u", G, et // 2), cast)
             tick()
 
         def U(G, ep, eng):
-            need(("u", G, 2 * ep))
-            need(("u", G, 2 * ep + 1))
+            need(("u", G, ep))
             ps = bank()
             for i in range(2):
-                words = ub[G, 2 * ep + i][:].bitcast(F32)
+                words = ub[G, ep][:].bitcast(F32)
                 for u in range(2):
                     o = 256 * i + 128 * u
-                    nc.tensor.transpose(ps[:, o : o + 128], words[:, 128 * u : 128 * (u + 1)], ident[:])
-            pg = work.tile([P, 256, 4], BF16, name="pg", tag="pg", bufs=3, align_bytes=64)
-            cols = slice(256 * ep, 256 * (ep + 1))
+                    w = 256 * u + 128 * i
+                    nc.tensor.transpose(ps[:, o : o + 128], words[:, w : w + 128], ident[:])
+            fine = G == 1 and ep >= 2
+            if fine or ep % 2 == 0:
+                pgs[G, ep // 2] = work.tile([P, 512, 4], BF16, name="pg", tag="pg", bufs=2, align_bytes=64)
+            o = 0 if fine else 256 * (ep % 2)
+            pg = pgs[G, ep // 2]
+            width = 256 if fine else 512
+            cols = slice(256 * ep, 256 * (ep + 1)) if fine else slice(256 * (ep - 1), 256 * (ep + 1))
 
             def evac():
-                dst = pg[:].bitcast(F32).rearrange("p (i e) u -> p i e u", i=2)
+                dst = pg[:, o : o + 256, :].bitcast(F32).rearrange("p (i e) u -> p i e u", i=2)
                 pcopy(eng, dst, ps[:].rearrange("p (i u e) -> p i e u", i=2, u=2))
 
             def quant():
                 nc.vector.quantize_mx(
-                    out=o_codes[:, G, cols].bitcast(X4), scales=o_sc[:, G, cols], in_=pg[:].rearrange("p e j -> p (e j)")
+                    out=o_codes[:, G, cols].bitcast(X4), scales=o_sc[:, G, cols], in_=pg[:, 0:width, :].rearrange("p e j -> p (e j)")
                 )
                 if ep % 2:
                     cc = slice(512 * (ep // 2), 512 * (ep // 2 + 1))
@@ -330,67 +474,13 @@ def tile_differencetargetpropweightstep_x2_kernel(tc, t, h, v_words, v_scales, b
                         )
 
             later(LT, ("o", G, ep), evac)
-            later(LQ, ("o", G, ep), quant)
+            if fine or ep % 2:
+                later(LQ, ("o", G, ep), quant)
             tick()
 
         BANKS = [(0, 0), (0, 1), (1, 0), (1, 1)]
-        for i, (jp, kg) in enumerate(BANKS):
-            T("t", 0, jp, kg, "VA"[i % 2])
-        load("t", 1)
-        BIAS()
-        for dt in range(8):
-            M("t", 0, dt)
-            if dt == 3:
-                X(0, 0)
-            if dt == 6:
-                X(0, 1)
-        load("h", 1)
-        for i, (jp, kg) in enumerate(BANKS):
-            T("h", 0, jp, kg, "VA"[i % 2])
-        load("a", 1)
-        tiles = [("t", 1, jp, kg) for jp, kg in BANKS] + [("h", 1, jp, kg) for jp, kg in BANKS]
-        for dt in range(0, 8, 2):
-            SIG(0, dt // 2)
-            M("h", 0, dt)
-            M("h", 0, dt + 1)
-            if dt == 0:
-                X(1, 0)
-            if dt == 2:
-                X(1, 1)
-            T(*tiles[dt], "A")
-            T(*tiles[dt + 1], "A")
-            if dt >= 2:
-                E(0, dt - 2)
-                E(0, dt - 1)
-        for dt in range(0, 8, 2):
-            SIG(1, dt // 2)
-            for i in range(2):
-                M("t", 1, dt + i)
-                M("h", 1, dt + i)
-            if dt == 0:
-                E(0, 6)
-                E(0, 7)
-            else:
-                E(1, dt - 2)
-                E(1, dt - 1)
-        for et in range(4):
-            S2(0, et, "A")
-        E(1, 6)
-        E(1, 7)
-        for et in range(4, 8):
-            S2(0, et, "A")
-        U(0, 0, "V")
-        U(0, 1, "V")
-        for et in range(4):
-            S2(1, et, "A")
-        U(0, 2, "V")
-        U(0, 3, "V")
-        for et in range(4, 8):
-            S2(1, et, "AV"[et % 2])
-        U(1, 0, "A")
-        U(1, 1, "V")
-        tick()
-        U(1, 2, "A")
-        U(1, 3, "V")
-        for i in range(8):
+        FN = {"T": T, "M": M, "E": E, "X": X, "SIG": SIG, "S2": S2, "U": U, "load": load, "loadv": loadv, "BIAS": BIAS, "tick": tick}
+        for f in PROG:
+            FN[f[0]](*f[1:])
+        for i in range(20):
             tick()

@@ -6,6 +6,7 @@ from concourse.masks import make_identity
 P = 128
 R = 1024
 FLOPS = 6 * R * R * R
+STORES = [[4, 8], [4, 6, 8]]
 
 F32 = mybir.dt.float32
 BF16 = mybir.dt.bfloat16
@@ -15,126 +16,134 @@ U8 = mybir.dt.uint8
 X4 = mybir.dt.float8_e4m3fn_x4
 ACT = mybir.ActivationFunctionType
 ALU = mybir.AluOpType
-LT = 1
+LT = 2
 LQ = 4
-LM = 1
-LS = 6
-LE = 3
-LEQ = 5
-LC = 7
-LX = 3
+LM = 3
+LS = 9
+LE = 4
+LEQ = 11
+LC = 9
+LX = 7
 LU = 2
-LUC = 5
-CENG = "V"
-ACCS = [[0,2],[0,4],[0,6],[1,4],[1,6],[1,2],[0,1]]
+LUC = 4
+ACCS = [[1,4],[1,6],[0,2],[0,7],[0,4],[1,2],[0,1]]
 PROG = [
-    ["load","t",0],
-    ["loadv"],
+    ["load","t",0,0],
+    ["load","t",0,1],
+    ["T0","VA"],
+    ["smallv"],
     ["load","x",0,0],
-    ["load","x",0,1],
-    ["T","t",0,0,1,"V"],
-    ["load","h",0],
-    ["T","t",0,0,0,"A"],
-    ["load","x",1],
     ["T","t",0,1,0,"A"],
-    ["load","a",0],
-    ["BIAS"],
-    ["T","t",0,1,1,"A"],
-    ["load","t",1],
-    ["M","t",0,3],
-    ["M","t",0,1],
-    ["load","h",1],
+    ["loadv"],
     ["X",0,0,"V"],
-    ["X",0,1,"V"],
-    ["M","t",0,4],
-    ["M","t",0,2],
-    ["M","t",0,5],
-    ["M","t",0,7],
-    ["X",1,0,"V"],
-    ["T","h",0,0,1,"V"],
+    ["load","x",0,1],
+    ["load","h",0,1],
+    ["T","t",0,1,1,"A"],
+    ["smallb"],
     ["M","t",0,0],
+    ["BIAS"],
+    ["load","h",0,0],
+    ["M","t",0,7],
+    ["M","t",0,5],
+    ["X",0,1,"V"],
+    ["M","t",0,1],
+    ["T","h",0,0,1,"V"],
+    ["load","x",1,0],
+    ["M","t",0,2],
+    ["load","a",0,1],
+    ["X",1,0,"V"],
     ["T","h",0,0,0,"A"],
     ["T","h",0,1,0,"A"],
-    ["SIG",0,0],
-    ["load","a",1],
     ["T","h",0,1,1,"V"],
+    ["load","t",1,1],
+    ["load","t",1,0],
+    ["M","t",0,3],
+    ["SIG",0,1,"V"],
     ["M","t",0,6],
-    ["M","h",0,0],
-    ["M","h",0,2],
-    ["X",1,1,"V"],
-    ["T","t",1,0,0,"A"],
-    ["T","t",1,1,0,"A"],
+    ["load","x",1,1],
     ["T","t",1,0,1,"V"],
-    ["M","h",0,1],
-    ["M","h",0,5],
-    ["M","h",0,3],
-    ["SIG",0,1],
     ["T","t",1,1,1,"V"],
-    ["T","h",1,0,1,"V"],
-    ["E",0,0],
+    ["T","t",1,0,0,"A"],
+    ["M","h",0,0],
+    ["X",1,1,"V"],
+    ["M","t",0,4],
+    ["M","h",0,5],
     ["M","h",0,4],
-    ["E",0,1],
+    ["load","a",0,0],
+    ["SIG",0,0,"V"],
+    ["M","h",0,6],
+    ["M","h",0,3],
+    ["load","h",1,0],
+    ["load","a",1,0],
+    ["load","h",1,1],
+    ["T","h",1,0,1,"A"],
+    ["T","t",1,1,0,"V"],
     ["T","h",1,0,0,"A"],
-    ["M","t",1,5],
+    ["M","h",0,1],
+    ["E",0,0],
     ["T","h",1,1,0,"A"],
-    ["T","h",1,1,1,"A"],
-    ["M","t",1,0],
     ["M","h",0,7],
+    ["M","h",0,2],
+    ["M","t",1,7],
     ["E",0,4],
     ["E",0,5],
-    ["SIG",1,0],
-    ["M","t",1,1],
-    ["M","h",1,0],
-    ["E",0,2],
-    ["E",0,3],
-    ["M","t",1,2],
-    ["M","h",0,6],
+    ["T","h",1,1,1,"V"],
     ["M","t",1,3],
-    ["M","h",1,1],
-    ["M","h",1,3],
-    ["E",0,7],
-    ["E",0,6],
-    ["E",1,0],
-    ["M","h",1,2],
-    ["M","h",1,5],
-    ["M","t",1,4],
-    ["M","h",1,4],
-    ["E",1,2],
-    ["E",1,3],
-    ["E",1,1],
-    ["SIG",1,1],
+    ["SIG",1,0,"V"],
+    ["E",0,1],
+    ["E",0,2],
+    ["load","a",1,1],
     ["M","t",1,6],
-    ["M","t",1,7],
+    ["M","t",1,0],
+    ["M","t",1,1],
+    ["M","h",1,1],
+    ["M","h",1,4],
+    ["E",0,3],
+    ["E",0,6],
+    ["E",0,7],
+    ["M","h",1,0],
+    ["M","h",1,3],
+    ["M","h",1,5],
+    ["M","h",1,2],
+    ["M","t",1,5],
+    ["M","t",1,2],
+    ["E",1,0],
+    ["M","t",1,4],
+    ["E",1,1],
+    ["E",1,3],
+    ["E",1,2],
+    ["SIG",1,1,"V"],
     ["M","h",1,7],
     ["M","h",1,6],
     ["E",1,4],
     ["E",1,5],
-    ["S2",0,0,"A"],
-    ["S2",0,1,"A"],
-    ["S2",0,2,"A"],
-    ["S2",0,3,"A"],
     ["S2",0,6,"A"],
+    ["S2",0,0,"A"],
+    ["S2",0,7,"A"],
+    ["S2",0,1,"A"],
+    ["S2",0,4,"A"],
+    ["S2",0,2,"A"],
     ["E",1,6],
     ["E",1,7],
-    ["S2",0,7,"A"],
-    ["S2",0,4,"A"],
+    ["S2",0,3,"A"],
     ["S2",0,5,"A"],
     ["U",0,0,"A"],
-    ["U",0,1,"V"],
     ["S2",1,6,"A"],
-    ["S2",1,2,"A"],
+    ["S2",1,2,"V"],
+    ["U",0,2,"A"],
+    ["U",0,4,"A"],
+    ["U",0,6,"A"],
     ["S2",1,3,"A"],
-    ["S2",1,0,"A"],
-    ["U",0,2,"V"],
-    ["U",0,3,"A"],
+    ["S2",1,0,"V"],
     ["S2",1,1,"A"],
-    ["S2",1,4,"A"],
-    ["S2",1,5,"A"],
+    ["S2",1,4,"V"],
     ["S2",1,7,"A"],
+    ["S2",1,5,"A"],
+    ["U",1,6,"A"],
     ["U",1,0,"A"],
-    ["U",1,1,"A"],
     ["U",1,2,"A"],
-    ["U",1,3,"A"],
+    ["U",1,4,"A"],
+    ["U",1,7,"A"],
 ]
 
 
@@ -188,19 +197,26 @@ def tile_differencetargetpropweightstep_x2_kernel(tc, t, h, v_words, v_scales, b
                 raw[op, g] = work.tile([P, 4, R], BF16, name="raw", tag="raw", bufs=6, align_bytes=64)
             view = src[op][512 * g : 512 * (g + 1), :].rearrange("(p j) f -> p j f", j=4)
             for i in range(2) if part is None else [part]:
-                if op == "x":
+                if op in "xa":
                     cols = slice(512 * i, 512 * (i + 1))
                     nc.sync.dma_start(out=raw[op, g][:, :, cols], in_=view[:, :, cols])
+                elif (op, g, i) == ("t", 0, 0):
+                    for j in range(2):
+                        nc.sync.dma_start(out=raw[op, g][:, j, :], in_=view[:, j, :])
                 else:
                     nc.sync.dma_start(out=raw[op, g][:, 2 * i : 2 * i + 2, :], in_=view[:, 2 * i : 2 * i + 2, :])
 
-        nc.scalar.dma_start(out=b_rows[0:8, :], in_=b.rearrange("(c p) -> c p", p=P))
-        for q in range(4):
-            nc.scalar.dma_start(
-                out=v_sc[32 * q : 32 * q + 4, :, :].bitcast(I32),
-                in_=v_scales[:, 4 * q : 4 * q + 4, :].rearrange("g q n -> q g n").bitcast(I32),
-            )
-        nc.scalar.dma_start(out=c_col[:], in_=c.rearrange("(g p j) -> p g j", g=2, j=4))
+        def smallb():
+            nc.gpsimd.dma_start(out=b_rows[0:8, :], in_=b.rearrange("(c p) -> c p", p=P))
+            nc.gpsimd.dma_start(out=c_col[:], in_=c.rearrange("(g p j) -> p g j", g=2, j=4))
+
+        def smallv():
+            for q in range(4):
+                nc.gpsimd.dma_start(
+                    out=v_sc[32 * q : 32 * q + 4, :, :].bitcast(I32),
+                    in_=v_scales[:, 4 * q : 4 * q + 4, :].rearrange("g q n -> q g n").bitcast(I32),
+                )
+
         nc.scalar.activation(warm[:, 1:2], warm[:, 0:1], ACT.Sigmoid)
         def loadv():
             for g in range(2):
@@ -273,6 +289,21 @@ def tile_differencetargetpropweightstep_x2_kernel(tc, t, h, v_words, v_scales, b
             later(LT, ("c", op, g), evac)
             if jp == 1:
                 later(LQ, ("c", op, g), quant)
+            tick()
+
+        def T0(engs):
+            banks = [bank(), bank()]
+            for kg in range(2):
+                grouped["t", 0, kg] = work.tile([P, 512, 4], BF16, name="gr", tag="gr", bufs=4, align_bytes=64)
+            for jj in range(2):
+                for kg in range(2):
+                    words = raw["t", 0][:, jj, 512 * kg : 512 * (kg + 1)].bitcast(F32)
+                    for u in range(2):
+                        o = 256 * jj + 128 * u
+                        nc.tensor.transpose(banks[kg][:, o : o + 128], words[:, u:256:2], ident[:])
+            for kg in range(2):
+                dst = grouped["t", 0, kg][:, 0:256, :].bitcast(F32).rearrange("p (j n) u -> p j n u", j=2)
+                pcopy(engs[kg], dst, banks[kg][:].rearrange("p (j u n) -> p j n u", j=2, u=2))
             tick()
 
         tanhs = {}
@@ -349,7 +380,7 @@ def tile_differencetargetpropweightstep_x2_kernel(tc, t, h, v_words, v_scales, b
                 later(LEQ, ("q", g, dt // 4), quant)
             tick()
 
-        def SIG(g, k):
+        def SIG(g, k, CENG="V"):
             cols = slice(512 * k, 512 * (k + 1))
             nc.scalar.activation(csig[g][:, :, cols], raw["a", g][:, :, cols], ACT.Sigmoid)
 
@@ -368,10 +399,12 @@ def tile_differencetargetpropweightstep_x2_kernel(tc, t, h, v_words, v_scales, b
         def X(g, half, XENG="V"):
             xg = work.tile([P, 512, 4], BF16, name="xg", tag="xg", bufs=2, align_bytes=64)
             cols = slice(512 * half, 512 * (half + 1))
+            dst = xg[:].rearrange("p (e i) j -> p e j i", i=4)
+            srcx = raw["x", g][:, :, cols].rearrange("p j (e i) -> p e j i", i=4)
             if XENG == "V":
-                nc.vector.tensor_copy(out=xg[:], in_=raw["x", g][:, :, cols].rearrange("p j e -> p e j"))
+                nc.vector.tensor_copy(out=dst, in_=srcx)
             elif XENG == "A":
-                nc.scalar.copy(out=xg[:], in_=raw["x", g][:, :, cols].rearrange("p j e -> p e j"))
+                nc.scalar.copy(out=dst, in_=srcx)
             else:
                 for i in range(4):
                     cc = slice(512 * half + 128 * i, 512 * half + 128 * (i + 1))
@@ -388,9 +421,11 @@ def tile_differencetargetpropweightstep_x2_kernel(tc, t, h, v_words, v_scales, b
 
             later(LX, ("x", g), quant)
 
-        ub = {}
         ufs = {}
-        pgs = {}
+        ub = {}
+
+        def unit(G, et):
+            return (et, 1) if G == 1 and et >= 6 else (et - et % 2, 2)
 
         def S2(G, et, eng):
             for g in range(2):
@@ -407,12 +442,13 @@ def tile_differencetargetpropweightstep_x2_kernel(tc, t, h, v_words, v_scales, b
                     start=(g == 0),
                     stop=(g == 1),
                 )
-            if et % 2 == 0:
-                ufs[G, et // 2] = work.tile([P, 2, 512], F32, name="uf", tag="uf", bufs=4, align_bytes=64)
-                ub[G, et // 2] = work.tile([P, 1024], BF16, name="u16", tag="u16", bufs=3, align_bytes=64)
-            uf = ufs[G, et // 2]
-            u16 = ub[G, et // 2]
-            i = et % 2
+            e0, n = unit(G, et)
+            if et == e0:
+                ufs[G, e0] = work.tile([P, 2, 512], F32, name="uf", tag="uf", bufs=4, align_bytes=64)
+                ub[G, e0] = work.tile([P, 1024], BF16, name="u16", tag="u16", bufs=4, align_bytes=64)
+            uf = ufs[G, e0]
+            u16 = ub[G, e0]
+            i = et - e0
 
             def evac():
                 if eng == "A":
@@ -422,64 +458,62 @@ def tile_differencetargetpropweightstep_x2_kernel(tc, t, h, v_words, v_scales, b
 
             def cast():
                 nc.vector.tensor_copy(
-                    out=u16[:].rearrange("e (u w i) -> e u w i", u=2, i=2),
-                    in_=uf[:].rearrange("e k (w u i) -> e u (k w) i", u=2, i=2),
+                    out=u16[:, 0 : 512 * n].rearrange("e (u w i) -> e u w i", u=2, i=2),
+                    in_=uf[:, 0:n, :].rearrange("e k (w u i) -> e u (k w) i", u=2, i=2),
                 )
                 nc.sync.dma_start(
-                    out=out_0[P * (et - 1) : P * (et + 1), 512 * G : 512 * (G + 1)].rearrange("(k e) d -> e k d", k=2),
-                    in_=uf[:],
+                    out=out_0[P * e0 : P * (e0 + n), 512 * G : 512 * (G + 1)].rearrange("(k e) d -> e k d", k=n),
+                    in_=uf[:, 0:n, :],
                 )
 
-            later(LU, ("u", G, et // 2), evac)
-            if i:
-                later(LUC, ("u", G, et // 2), cast)
+            later(LU, ("u", G, e0), evac)
+            if i == n - 1:
+                later(LUC, ("u", G, e0), cast)
             tick()
 
-        def U(G, ep, eng):
-            need(("u", G, ep))
+        def U(G, e0, eng):
+            need(("u", G, e0))
+            n = unit(G, e0)[1]
             ps = bank()
-            for i in range(2):
-                words = ub[G, ep][:].bitcast(F32)
+            words = ub[G, e0][:, 0 : 512 * n].bitcast(F32)
+            for i in range(n):
                 for u in range(2):
                     o = 256 * i + 128 * u
-                    w = 256 * u + 128 * i
+                    w = 128 * n * u + 128 * i
                     nc.tensor.transpose(ps[:, o : o + 128], words[:, w : w + 128], ident[:])
-            fine = G == 1 and ep >= 2
-            if fine or ep % 2 == 0:
-                pgs[G, ep // 2] = work.tile([P, 512, 4], BF16, name="pg", tag="pg", bufs=2, align_bytes=64)
-            o = 0 if fine else 256 * (ep % 2)
-            pg = pgs[G, ep // 2]
-            width = 256 if fine else 512
-            cols = slice(256 * ep, 256 * (ep + 1)) if fine else slice(256 * (ep - 1), 256 * (ep + 1))
+            pg = work.tile([P, 256, 4], BF16, name="pg", tag="pg", bufs=4, align_bytes=64)
+            cols = slice(P * e0, P * (e0 + n))
 
             def evac():
-                dst = pg[:, o : o + 256, :].bitcast(F32).rearrange("p (i e) u -> p i e u", i=2)
-                pcopy(eng, dst, ps[:].rearrange("p (i u e) -> p i e u", i=2, u=2))
+                dst = pg[:, 0 : P * n, :].bitcast(F32).rearrange("p (i e) u -> p i e u", i=n)
+                pcopy(eng, dst, ps[:, 0 : 256 * n].rearrange("p (i u e) -> p i e u", i=n, u=2))
 
             def quant():
                 nc.vector.quantize_mx(
-                    out=o_codes[:, G, cols].bitcast(X4), scales=o_sc[:, G, cols], in_=pg[:, 0:width, :].rearrange("p e j -> p (e j)")
+                    out=o_codes[:, G, cols].bitcast(X4),
+                    scales=o_sc[:, G, cols],
+                    in_=pg[:, 0 : P * n, :].rearrange("p e j -> p (e j)"),
                 )
-                if ep % 2:
-                    cc = slice(512 * (ep // 2), 512 * (ep // 2 + 1))
+                last = e0 + n
+                if last in STORES[G]:
+                    k = STORES[G].index(last)
+                    cc = slice(P * (STORES[G][k - 1] if k else 0), P * last)
                     nc.sync.dma_start(
                         out=out_1[G, :, cc, :].rearrange("p m t -> p (m t)").bitcast(I32),
                         in_=o_codes[:, G, cc].bitcast(I32),
                     )
-                if ep == 3:
+                if last == 8:
                     for q in range(4):
-                        nc.sync.dma_start(
+                        nc.scalar.dma_start(
                             out=out_2[G, 4 * q : 4 * q + 4, :].bitcast(I32),
                             in_=o_sc[32 * q : 32 * q + 4, G, :].bitcast(I32),
                         )
 
-            later(LT, ("o", G, ep), evac)
-            if fine or ep % 2:
-                later(LQ, ("o", G, ep), quant)
+            later(LT, ("o", G, e0), evac)
+            later(LQ, ("o", G, e0), quant)
             tick()
 
-        BANKS = [(0, 0), (0, 1), (1, 0), (1, 1)]
-        FN = {"T": T, "M": M, "E": E, "X": X, "SIG": SIG, "S2": S2, "U": U, "load": load, "loadv": loadv, "BIAS": BIAS, "tick": tick}
+        FN = {"smallb": smallb, "smallv": smallv, "T": T, "T0": T0, "M": M, "E": E, "X": X, "SIG": SIG, "S2": S2, "U": U, "load": load, "loadv": loadv, "BIAS": BIAS, "tick": tick}
         for f in PROG:
             FN[f[0]](*f[1:])
         for i in range(20):

@@ -16,132 +16,133 @@ U8 = mybir.dt.uint8
 X4 = mybir.dt.float8_e4m3fn_x4
 ACT = mybir.ActivationFunctionType
 ALU = mybir.AluOpType
-LT = 2
+LT = 1
 LQ = 4
-LM = 3
-LS = 9
+LM = 2
+LS = 5
 LE = 4
-LEQ = 11
-LC = 9
-LX = 7
+LEQ = 12
+LC = 6
+LX = 3
 LU = 2
 LUC = 4
-ACCS = [[1,4],[1,6],[0,2],[0,7],[0,4],[1,2],[0,1]]
+ACCS = [[0,4],[1,2],[1,5],[1,7],[0,5],[1,0]]
 PROG = [
     ["load","t",0,0],
     ["load","t",0,1],
     ["T0","VA"],
-    ["smallv"],
-    ["load","x",0,0],
+    ["smallc"],
     ["T","t",0,1,0,"A"],
-    ["loadv"],
+    ["load","x",0,0],
     ["X",0,0,"V"],
-    ["load","x",0,1],
-    ["load","h",0,1],
     ["T","t",0,1,1,"A"],
     ["smallb"],
-    ["M","t",0,0],
-    ["BIAS"],
+    ["loadv"],
+    ["smallv"],
     ["load","h",0,0],
-    ["M","t",0,7],
-    ["M","t",0,5],
-    ["X",0,1,"V"],
-    ["M","t",0,1],
-    ["T","h",0,0,1,"V"],
-    ["load","x",1,0],
-    ["M","t",0,2],
-    ["load","a",0,1],
-    ["X",1,0,"V"],
-    ["T","h",0,0,0,"A"],
-    ["T","h",0,1,0,"A"],
-    ["T","h",0,1,1,"V"],
-    ["load","t",1,1],
-    ["load","t",1,0],
-    ["M","t",0,3],
-    ["SIG",0,1,"V"],
-    ["M","t",0,6],
-    ["load","x",1,1],
-    ["T","t",1,0,1,"V"],
-    ["T","t",1,1,1,"V"],
-    ["T","t",1,0,0,"A"],
-    ["M","h",0,0],
-    ["X",1,1,"V"],
+    ["BIAS"],
+    ["load","h",0,1],
     ["M","t",0,4],
-    ["M","h",0,5],
-    ["M","h",0,4],
-    ["load","a",0,0],
-    ["SIG",0,0,"V"],
-    ["M","h",0,6],
-    ["M","h",0,3],
+    ["M","t",0,2],
+    ["M","t",0,5],
+    ["load","x",0,1],
+    ["X",0,1,"V"],
+    ["load","x",1,0],
+    ["load","x",1,1],
+    ["load","a",0,1],
+    ["T","h",0,0,0,"A"],
+    ["load","t",1,0],
+    ["T","h",0,1,0,"A"],
     ["load","h",1,0],
-    ["load","a",1,0],
+    ["load","t",1,1],
+    ["X",1,0,"V"],
+    ["T","h",0,0,1,"A"],
+    ["M","t",0,1],
+    ["T","h",0,1,1,"A"],
+    ["load","a",0,0],
+    ["SIG",0,1,"V"],
+    ["M","t",0,3],
+    ["M","t",0,7],
     ["load","h",1,1],
-    ["T","h",1,0,1,"A"],
-    ["T","t",1,1,0,"V"],
+    ["X",1,1,"V"],
+    ["M","t",0,0],
+    ["T","t",1,0,0,"V"],
+    ["T","t",1,0,1,"V"],
     ["T","h",1,0,0,"A"],
     ["M","h",0,1],
+    ["M","h",0,0],
+    ["T","t",1,1,0,"V"],
+    ["load","a",1,0],
+    ["M","h",0,3],
+    ["M","t",0,6],
+    ["T","h",1,0,1,"V"],
+    ["T","t",1,1,1,"A"],
+    ["T","h",1,1,1,"A"],
+    ["M","h",0,4],
+    ["T","h",1,1,0,"V"],
     ["E",0,0],
-    ["T","h",1,1,0,"A"],
-    ["M","h",0,7],
     ["M","h",0,2],
-    ["M","t",1,7],
-    ["E",0,4],
-    ["E",0,5],
-    ["T","h",1,1,1,"V"],
-    ["M","t",1,3],
-    ["SIG",1,0,"V"],
-    ["E",0,1],
-    ["E",0,2],
+    ["SIG",0,0,"V"],
+    ["M","h",0,5],
     ["load","a",1,1],
-    ["M","t",1,6],
-    ["M","t",1,0],
+    ["M","h",0,6],
     ["M","t",1,1],
+    ["M","t",1,7],
+    ["E",0,3],
+    ["E",0,4],
+    ["E",0,1],
+    ["M","h",0,7],
+    ["M","h",1,0],
+    ["E",0,2],
+    ["SIG",1,0,"V"],
+    ["E",0,5],
+    ["M","t",1,4],
+    ["M","t",1,3],
+    ["M","t",1,0],
     ["M","h",1,1],
     ["M","h",1,4],
-    ["E",0,3],
-    ["E",0,6],
-    ["E",0,7],
-    ["M","h",1,0],
     ["M","h",1,3],
     ["M","h",1,5],
-    ["M","h",1,2],
-    ["M","t",1,5],
-    ["M","t",1,2],
+    ["M","t",1,6],
+    ["E",0,6],
+    ["E",0,7],
     ["E",1,0],
-    ["M","t",1,4],
-    ["E",1,1],
+    ["M","h",1,2],
+    ["M","t",1,2],
+    ["M","t",1,5],
     ["E",1,3],
-    ["E",1,2],
+    ["E",1,1],
     ["SIG",1,1,"V"],
-    ["M","h",1,7],
+    ["E",1,2],
     ["M","h",1,6],
     ["E",1,4],
     ["E",1,5],
+    ["M","h",1,7],
     ["S2",0,6,"A"],
     ["S2",0,0,"A"],
     ["S2",0,7,"A"],
     ["S2",0,1,"A"],
-    ["S2",0,4,"A"],
     ["S2",0,2,"A"],
-    ["E",1,6],
     ["E",1,7],
+    ["E",1,6],
+    ["S2",0,4,"A"],
     ["S2",0,3,"A"],
     ["S2",0,5,"A"],
     ["U",0,0,"A"],
-    ["S2",1,6,"A"],
-    ["S2",1,2,"V"],
+    ["S2",1,6,"V"],
     ["U",0,2,"A"],
     ["U",0,4,"A"],
     ["U",0,6,"A"],
+    ["S2",1,0,"A"],
+    ["S2",1,1,"V"],
+    ["S2",1,2,"A"],
     ["S2",1,3,"A"],
-    ["S2",1,0,"V"],
-    ["S2",1,1,"A"],
-    ["S2",1,4,"V"],
-    ["S2",1,7,"A"],
+    ["S2",1,4,"A"],
     ["S2",1,5,"A"],
-    ["U",1,6,"A"],
+    ["S2",1,7,"V"],
     ["U",1,0,"A"],
     ["U",1,2,"A"],
+    ["U",1,6,"A"],
     ["U",1,4,"A"],
     ["U",1,7,"A"],
 ]
@@ -207,12 +208,14 @@ def tile_differencetargetpropweightstep_x2_kernel(tc, t, h, v_words, v_scales, b
                     nc.sync.dma_start(out=raw[op, g][:, 2 * i : 2 * i + 2, :], in_=view[:, 2 * i : 2 * i + 2, :])
 
         def smallb():
-            nc.gpsimd.dma_start(out=b_rows[0:8, :], in_=b.rearrange("(c p) -> c p", p=P))
-            nc.gpsimd.dma_start(out=c_col[:], in_=c.rearrange("(g p j) -> p g j", g=2, j=4))
+            nc.sync.dma_start(out=b_rows[0:8, :], in_=b.rearrange("(c p) -> c p", p=P))
+
+        def smallc():
+            nc.sync.dma_start(out=c_col[:], in_=c.rearrange("(g p j) -> p g j", g=2, j=4))
 
         def smallv():
             for q in range(4):
-                nc.gpsimd.dma_start(
+                nc.sync.dma_start(
                     out=v_sc[32 * q : 32 * q + 4, :, :].bitcast(I32),
                     in_=v_scales[:, 4 * q : 4 * q + 4, :].rearrange("g q n -> q g n").bitcast(I32),
                 )
@@ -504,7 +507,7 @@ def tile_differencetargetpropweightstep_x2_kernel(tc, t, h, v_words, v_scales, b
                     )
                 if last == 8:
                     for q in range(4):
-                        nc.scalar.dma_start(
+                        nc.sync.dma_start(
                             out=out_2[G, 4 * q : 4 * q + 4, :].bitcast(I32),
                             in_=o_sc[32 * q : 32 * q + 4, G, :].bitcast(I32),
                         )
@@ -513,7 +516,7 @@ def tile_differencetargetpropweightstep_x2_kernel(tc, t, h, v_words, v_scales, b
             later(LQ, ("o", G, e0), quant)
             tick()
 
-        FN = {"smallb": smallb, "smallv": smallv, "T": T, "T0": T0, "M": M, "E": E, "X": X, "SIG": SIG, "S2": S2, "U": U, "load": load, "loadv": loadv, "BIAS": BIAS, "tick": tick}
+        FN = {"smallb": smallb, "smallc": smallc, "smallv": smallv, "T": T, "T0": T0, "M": M, "E": E, "X": X, "SIG": SIG, "S2": S2, "U": U, "load": load, "loadv": loadv, "BIAS": BIAS, "tick": tick}
         for f in PROG:
             FN[f[0]](*f[1:])
         for i in range(20):

@@ -16,135 +16,131 @@ U8 = mybir.dt.uint8
 X4 = mybir.dt.float8_e4m3fn_x4
 ACT = mybir.ActivationFunctionType
 ALU = mybir.AluOpType
-LT = 1
-LQ = 4
-LM = 2
-LS = 5
+LT = 3
+LQ = 5
+LM = 3
+LS = 12
 LE = 4
-LEQ = 12
-LC = 6
-LX = 3
-LU = 2
-LUC = 4
-ACCS = [[0,4],[1,2],[1,5],[1,7],[0,5],[1,0]]
+LEQ = 18
+LC = 7
+LX = 4
+LU = 4
+LUC = 7
+ACCS = [[1,5],[1,1],[1,7],[1,0],[0,5],[0,4]]
 PROG = [
     ["load","t",0,0],
+    ["smallv"],
+    ["smallb"],
     ["load","t",0,1],
     ["T0","VA"],
-    ["smallc"],
-    ["T","t",0,1,0,"A"],
-    ["load","x",0,0],
-    ["X",0,0,"V"],
-    ["T","t",0,1,1,"A"],
-    ["smallb"],
-    ["loadv"],
-    ["smallv"],
     ["load","h",0,0],
+    ["T","t",0,1,1,"V"],
     ["BIAS"],
+    ["T","t",0,1,0,"A"],
+    ["T","h",0,0,0,"V"],
+    ["loadv"],
+    ["T","h",0,0,1,"A"],
+    ["load","x",0],
     ["load","h",0,1],
     ["M","t",0,4],
-    ["M","t",0,2],
     ["M","t",0,5],
-    ["load","x",0,1],
-    ["X",0,1,"V"],
-    ["load","x",1,0],
-    ["load","x",1,1],
-    ["load","a",0,1],
-    ["T","h",0,0,0,"A"],
     ["load","t",1,0],
-    ["T","h",0,1,0,"A"],
-    ["load","h",1,0],
-    ["load","t",1,1],
-    ["X",1,0,"V"],
-    ["T","h",0,0,1,"A"],
-    ["M","t",0,1],
-    ["T","h",0,1,1,"A"],
-    ["load","a",0,0],
-    ["SIG",0,1,"V"],
-    ["M","t",0,3],
-    ["M","t",0,7],
-    ["load","h",1,1],
-    ["X",1,1,"V"],
+    ["load","x",1],
     ["M","t",0,0],
-    ["T","t",1,0,0,"V"],
-    ["T","t",1,0,1,"V"],
-    ["T","h",1,0,0,"A"],
-    ["M","h",0,1],
+    ["X",0,1,"V"],
+    ["load","a",0],
+    ["M","t",0,3],
+    ["T","h",0,1,0,"A"],
+    ["X",0,0,"V"],
+    ["T","h",0,1,1,"A"],
+    ["M","t",0,7],
+    ["load","h",1,0],
+    ["T","t",1,0,0,"A"],
+    ["smallc"],
     ["M","h",0,0],
-    ["T","t",1,1,0,"V"],
-    ["load","a",1,0],
+    ["M","t",0,1],
+    ["X",1,1,"V"],
+    ["M","t",0,2],
+    ["M","h",0,2],
+    ["X",1,0,"V"],
     ["M","h",0,3],
+    ["load","t",1,1],
+    ["T","t",1,0,1,"V"],
+    ["load","h",1,1],
+    ["SIG",0,1,"V"],
+    ["M","h",0,1],
+    ["M","h",0,4],
+    ["T","h",1,0,0,"A"],
     ["M","t",0,6],
     ["T","h",1,0,1,"V"],
-    ["T","t",1,1,1,"A"],
-    ["T","h",1,1,1,"A"],
-    ["M","h",0,4],
-    ["T","h",1,1,0,"V"],
-    ["E",0,0],
-    ["M","h",0,2],
     ["SIG",0,0,"V"],
+    ["T","t",1,1,0,"V"],
+    ["T","t",1,1,1,"V"],
     ["M","h",0,5],
-    ["load","a",1,1],
-    ["M","h",0,6],
-    ["M","t",1,1],
-    ["M","t",1,7],
-    ["E",0,3],
-    ["E",0,4],
-    ["E",0,1],
+    ["T","h",1,1,1,"A"],
+    ["T","h",1,1,0,"A"],
+    ["E",0,0],
     ["M","h",0,7],
-    ["M","h",1,0],
+    ["M","h",0,6],
+    ["E",0,3],
+    ["M","t",1,1],
+    ["E",0,1],
     ["E",0,2],
-    ["SIG",1,0,"V"],
-    ["E",0,5],
-    ["M","t",1,4],
-    ["M","t",1,3],
+    ["E",0,4],
     ["M","t",1,0],
-    ["M","h",1,1],
-    ["M","h",1,4],
+    ["M","t",1,3],
     ["M","h",1,3],
-    ["M","h",1,5],
-    ["M","t",1,6],
-    ["E",0,6],
-    ["E",0,7],
-    ["E",1,0],
+    ["load","a",1],
     ["M","h",1,2],
+    ["SIG",1,0,"V"],
+    ["M","h",1,0],
     ["M","t",1,2],
+    ["M","h",1,4],
+    ["M","t",1,4],
+    ["E",0,5],
+    ["E",0,7],
+    ["M","t",1,7],
+    ["M","t",1,6],
+    ["M","h",1,1],
+    ["E",1,0],
+    ["E",0,6],
+    ["M","h",1,5],
     ["M","t",1,5],
-    ["E",1,3],
+    ["E",1,2],
     ["E",1,1],
     ["SIG",1,1,"V"],
-    ["E",1,2],
     ["M","h",1,6],
+    ["E",1,3],
     ["E",1,4],
     ["E",1,5],
     ["M","h",1,7],
-    ["S2",0,6,"A"],
     ["S2",0,0,"A"],
-    ["S2",0,7,"A"],
-    ["S2",0,1,"A"],
     ["S2",0,2,"A"],
+    ["S2",0,1,"A"],
     ["E",1,7],
-    ["E",1,6],
-    ["S2",0,4,"A"],
     ["S2",0,3,"A"],
+    ["S2",0,4,"A"],
+    ["S2",0,6,"A"],
+    ["S2",0,7,"A"],
+    ["E",1,6],
     ["S2",0,5,"A"],
     ["U",0,0,"A"],
-    ["S2",1,6,"V"],
     ["U",0,2,"A"],
+    ["S2",1,0,"A"],
+    ["S2",1,1,"A"],
+    ["S2",1,4,"A"],
+    ["S2",1,5,"V"],
+    ["S2",1,6,"A"],
     ["U",0,4,"A"],
     ["U",0,6,"A"],
-    ["S2",1,0,"A"],
-    ["S2",1,1,"V"],
     ["S2",1,2,"A"],
     ["S2",1,3,"A"],
-    ["S2",1,4,"A"],
-    ["S2",1,5,"A"],
-    ["S2",1,7,"V"],
+    ["U",1,4,"V"],
+    ["S2",1,7,"A"],
+    ["U",1,6,"V"],
     ["U",1,0,"A"],
     ["U",1,2,"A"],
-    ["U",1,6,"A"],
-    ["U",1,4,"A"],
-    ["U",1,7,"A"],
+    ["U",1,7,"V"],
 ]
 
 
@@ -197,15 +193,14 @@ def tile_differencetargetpropweightstep_x2_kernel(tc, t, h, v_words, v_scales, b
             if (op, g) not in raw:
                 raw[op, g] = work.tile([P, 4, R], BF16, name="raw", tag="raw", bufs=6, align_bytes=64)
             view = src[op][512 * g : 512 * (g + 1), :].rearrange("(p j) f -> p j f", j=4)
-            for i in range(2) if part is None else [part]:
-                if op in "xa":
-                    cols = slice(512 * i, 512 * (i + 1))
-                    nc.sync.dma_start(out=raw[op, g][:, :, cols], in_=view[:, :, cols])
-                elif (op, g, i) == ("t", 0, 0):
-                    for j in range(2):
-                        nc.sync.dma_start(out=raw[op, g][:, j, :], in_=view[:, j, :])
-                else:
-                    nc.sync.dma_start(out=raw[op, g][:, 2 * i : 2 * i + 2, :], in_=view[:, 2 * i : 2 * i + 2, :])
+            if op in "xa":
+                nc.sync.dma_start(out=raw[op, g][:], in_=view)
+                return
+            if (op, g, part) == ("t", 0, 0):
+                for j in range(2):
+                    nc.sync.dma_start(out=raw[op, g][:, j, :], in_=view[:, j, :])
+                return
+            nc.sync.dma_start(out=raw[op, g][:, 2 * part : 2 * part + 2, :], in_=view[:, 2 * part : 2 * part + 2, :])
 
         def smallb():
             nc.sync.dma_start(out=b_rows[0:8, :], in_=b.rearrange("(c p) -> c p", p=P))
@@ -402,8 +397,8 @@ def tile_differencetargetpropweightstep_x2_kernel(tc, t, h, v_words, v_scales, b
         def X(g, half, XENG="V"):
             xg = work.tile([P, 512, 4], BF16, name="xg", tag="xg", bufs=2, align_bytes=64)
             cols = slice(512 * half, 512 * (half + 1))
-            dst = xg[:].rearrange("p (e i) j -> p e j i", i=4)
-            srcx = raw["x", g][:, :, cols].rearrange("p j (e i) -> p e j i", i=4)
+            dst = xg[:]
+            srcx = raw["x", g][:, :, cols].rearrange("p j e -> p e j")
             if XENG == "V":
                 nc.vector.tensor_copy(out=dst, in_=srcx)
             elif XENG == "A":

from contextlib import ExitStack

import concourse.mybir as mybir
from concourse.masks import make_identity

P = 128
R = 1024
FLOPS = 6 * R * R * R
STORES = [[4, 8], [4, 6, 8]]

F32 = mybir.dt.float32
BF16 = mybir.dt.bfloat16
I32 = mybir.dt.int32
U32 = mybir.dt.uint32
U8 = mybir.dt.uint8
X4 = mybir.dt.float8_e4m3fn_x4
ACT = mybir.ActivationFunctionType
ALU = mybir.AluOpType
LT = 3
LQ = 5
LM = 3
LS = 12
LE = 4
LEQ = 18
LC = 7
LX = 4
LU = 4
LUC = 7
ACCS = [[1,5],[1,1],[1,7],[1,0],[0,5],[0,4]]
PROG = [
    ["load","t",0,0],
    ["smallv"],
    ["smallb"],
    ["load","t",0,1],
    ["T0","VA"],
    ["load","h",0,0],
    ["T","t",0,1,1,"V"],
    ["BIAS"],
    ["T","t",0,1,0,"A"],
    ["T","h",0,0,0,"V"],
    ["loadv"],
    ["T","h",0,0,1,"A"],
    ["load","x",0],
    ["load","h",0,1],
    ["M","t",0,4],
    ["M","t",0,5],
    ["load","t",1,0],
    ["load","x",1],
    ["M","t",0,0],
    ["X",0,1,"V"],
    ["load","a",0],
    ["M","t",0,3],
    ["T","h",0,1,0,"A"],
    ["X",0,0,"V"],
    ["T","h",0,1,1,"A"],
    ["M","t",0,7],
    ["load","h",1,0],
    ["T","t",1,0,0,"A"],
    ["smallc"],
    ["M","h",0,0],
    ["M","t",0,1],
    ["X",1,1,"V"],
    ["M","t",0,2],
    ["M","h",0,2],
    ["X",1,0,"V"],
    ["M","h",0,3],
    ["load","t",1,1],
    ["T","t",1,0,1,"V"],
    ["load","h",1,1],
    ["SIG",0,1,"V"],
    ["M","h",0,1],
    ["M","h",0,4],
    ["T","h",1,0,0,"A"],
    ["M","t",0,6],
    ["T","h",1,0,1,"V"],
    ["SIG",0,0,"V"],
    ["T","t",1,1,0,"V"],
    ["T","t",1,1,1,"V"],
    ["M","h",0,5],
    ["T","h",1,1,1,"A"],
    ["T","h",1,1,0,"A"],
    ["E",0,0],
    ["M","h",0,7],
    ["M","h",0,6],
    ["E",0,3],
    ["M","t",1,1],
    ["E",0,1],
    ["E",0,2],
    ["E",0,4],
    ["M","t",1,0],
    ["M","t",1,3],
    ["M","h",1,3],
    ["load","a",1],
    ["M","h",1,2],
    ["SIG",1,0,"V"],
    ["M","h",1,0],
    ["M","t",1,2],
    ["M","h",1,4],
    ["M","t",1,4],
    ["E",0,5],
    ["E",0,7],
    ["M","t",1,7],
    ["M","t",1,6],
    ["M","h",1,1],
    ["E",1,0],
    ["E",0,6],
    ["M","h",1,5],
    ["M","t",1,5],
    ["E",1,2],
    ["E",1,1],
    ["SIG",1,1,"V"],
    ["M","h",1,6],
    ["E",1,3],
    ["E",1,4],
    ["E",1,5],
    ["M","h",1,7],
    ["S2",0,0,"A"],
    ["S2",0,2,"A"],
    ["S2",0,1,"A"],
    ["E",1,7],
    ["S2",0,3,"A"],
    ["S2",0,4,"A"],
    ["S2",0,6,"A"],
    ["S2",0,7,"A"],
    ["E",1,6],
    ["S2",0,5,"A"],
    ["U",0,0,"A"],
    ["U",0,2,"A"],
    ["S2",1,0,"A"],
    ["S2",1,1,"A"],
    ["S2",1,4,"A"],
    ["S2",1,5,"V"],
    ["S2",1,6,"A"],
    ["U",0,4,"A"],
    ["U",0,6,"A"],
    ["S2",1,2,"A"],
    ["S2",1,3,"A"],
    ["U",1,4,"V"],
    ["S2",1,7,"A"],
    ["U",1,6,"V"],
    ["U",1,0,"A"],
    ["U",1,2,"A"],
    ["U",1,7,"V"],
]


def ACC(g, dt):
    return [g, dt] in ACCS


def tile_differencetargetpropweightstep_x2_kernel(tc, t, h, v_words, v_scales, b, a, x, c, out_0, out_1, out_2):
    nc = tc.nc
    with ExitStack() as ctx:
        keep = ctx.enter_context(tc.tile_pool(name="keep", bufs=1))
        work = ctx.enter_context(tc.tile_pool(name="work", bufs=2))
        psum = ctx.enter_context(tc.psum_pool(name="psum", bufs=8))

        def bank():
            return psum.tile([P, 512], F32, name="ps", tag="ps", bufs=8)

        ctx.enter_context(tc.manual_schedule())
        ident = keep.tile([P, P], F32, name="ident", align_bytes=64)
        warm = keep.tile([P, 2], F32, name="warm")
        v_codes = keep.tile([P, 2, R], U32, name="v_codes", align_bytes=64)
        v_sc = keep.tile([P, 2, R], U8, name="v_sc", align_bytes=64)
        b_rows = keep.tile([P, P], BF16, name="b_rows")
        b_rows32 = keep.tile([P, P], F32, name="b_rows32", align_bytes=64)
        b_col = keep.tile([P, 8], F32, name="b_col")
        c_col = keep.tile([P, 2, 4], BF16, name="c_col")
        x_codes = keep.tile([P, 2, R], U32, name="x_codes", align_bytes=64)
        x_sc = keep.tile([P, 2, R], U8, name="x_sc", align_bytes=64)
        q_codes = keep.tile([P, 2, R], U32, name="q_codes", align_bytes=64)
        q_sc = keep.tile([P, 2, R], U8, name="q_sc", align_bytes=64)
        o_codes = keep.tile([P, 2, R], U32, name="o_codes", align_bytes=64)
        o_sc = keep.tile([P, 2, R], U8, name="o_sc", align_bytes=64)
        codes = {}
        scales = {}
        for op in "th":
            for g in range(2):
                codes[op, g] = keep.tile([P, 2, 512], U32, name="codes_%s%d" % (op, g), align_bytes=64)
                scales[op, g] = keep.tile([P, 2, 512], U8, name="scales_%s%d" % (op, g), align_bytes=64)
        csig = [keep.tile([P, 4, R], F32, name="csig%d" % g, align_bytes=64) for g in range(2)]

        nc.vector.memset(v_sc[:].rearrange("p g n -> p (g n)").bitcast(I32), 0)
        nc.vector.memset(b_rows[:], 0.0)
        nc.vector.memset(warm[:], 0.0)
        make_identity(nc, ident[:])

        src = {"t": t, "h": h, "x": x, "a": a}
        raw = {}

        def load(op, g, part=None):
            if (op, g) not in raw:
                raw[op, g] = work.tile([P, 4, R], BF16, name="raw", tag="raw", bufs=6, align_bytes=64)
            view = src[op][512 * g : 512 * (g + 1), :].rearrange("(p j) f -> p j f", j=4)
            if op in "xa":
                nc.sync.dma_start(out=raw[op, g][:], in_=view)
                return
            if (op, g, part) == ("t", 0, 0):
                for j in range(2):
                    nc.sync.dma_start(out=raw[op, g][:, j, :], in_=view[:, j, :])
                return
            nc.sync.dma_start(out=raw[op, g][:, 2 * part : 2 * part + 2, :], in_=view[:, 2 * part : 2 * part + 2, :])

        def smallb():
            nc.sync.dma_start(out=b_rows[0:8, :], in_=b.rearrange("(c p) -> c p", p=P))

        def smallc():
            nc.sync.dma_start(out=c_col[:], in_=c.rearrange("(g p j) -> p g j", g=2, j=4))

        def smallv():
            for q in range(4):
                nc.sync.dma_start(
                    out=v_sc[32 * q : 32 * q + 4, :, :].bitcast(I32),
                    in_=v_scales[:, 4 * q : 4 * q + 4, :].rearrange("g q n -> q g n").bitcast(I32),
                )

        nc.scalar.activation(warm[:, 1:2], warm[:, 0:1], ACT.Sigmoid)
        def loadv():
            for g in range(2):
                nc.sync.dma_start(
                    out=v_codes[:, g, :].bitcast(I32), in_=v_words[g].rearrange("p n t -> p (n t)").bitcast(I32)
                )


        nb_col = keep.tile([P, 8], F32, name="nb_col")

        def BIAS():
            nc.vector.tensor_copy(out=b_rows32[:], in_=b_rows[:])
            bp = bank()
            nc.tensor.transpose(bp[:, 0:P], b_rows32[:], ident[:])
            nc.vector.tensor_copy(out=b_col[:], in_=bp[:, 0:8])
            nc.vector.tensor_scalar(out=nb_col[:], in0=b_col[:], scalar1=-1.0, scalar2=None, op0=ALU.mult)

        pending = []

        def later(n, key, fn):
            pending.append([n, key, fn])

        def tick():
            due = []
            for item in pending:
                item[0] -= 1
                if item[0] <= 0:
                    due.append(item)
            for item in due:
                if item in pending:
                    pending.remove(item)
                    item[2]()

        def need(key):
            for item in list(pending):
                if item[1] == key:
                    pending.remove(item)
                    item[2]()

        grouped = {}

        def pcopy(eng, dst, srcv):
            if eng == "V":
                nc.vector.tensor_copy(out=dst, in_=srcv)
            else:
                nc.scalar.copy(out=dst, in_=srcv)

        def T(op, g, jp, kg, eng):
            ps = bank()
            for jj in range(2):
                words = raw[op, g][:, 2 * jp + jj, 512 * kg : 512 * (kg + 1)].bitcast(F32)
                for u in range(2):
                    o = 256 * jj + 128 * u
                    nc.tensor.transpose(ps[:, o : o + 128], words[:, u:256:2], ident[:])
            if jp == 0:
                grouped[op, g, kg] = work.tile([P, 512, 4], BF16, name="gr", tag="gr", bufs=4, align_bytes=64)
            gr = grouped[op, g, kg]

            def evac():
                dst = gr[:, 256 * jp : 256 * (jp + 1), :].bitcast(F32).rearrange("p (j n) u -> p j n u", j=2)
                pcopy(eng, dst, ps[:].rearrange("p (j u n) -> p j n u", j=2, u=2))

            def quant():
                nc.vector.quantize_mx(
                    out=codes[op, g][:, kg, :].bitcast(X4),
                    scales=scales[op, g][:, kg, :],
                    in_=gr[:].rearrange("p n k -> p (n k)"),
                )

            later(LT, ("c", op, g), evac)
            if jp == 1:
                later(LQ, ("c", op, g), quant)
            tick()

        def T0(engs):
            banks = [bank(), bank()]
            for kg in range(2):
                grouped["t", 0, kg] = work.tile([P, 512, 4], BF16, name="gr", tag="gr", bufs=4, align_bytes=64)
            for jj in range(2):
                for kg in range(2):
                    words = raw["t", 0][:, jj, 512 * kg : 512 * (kg + 1)].bitcast(F32)
                    for u in range(2):
                        o = 256 * jj + 128 * u
                        nc.tensor.transpose(banks[kg][:, o : o + 128], words[:, u:256:2], ident[:])
            for kg in range(2):
                dst = grouped["t", 0, kg][:, 0:256, :].bitcast(F32).rearrange("p (j n) u -> p j n u", j=2)
                pcopy(engs[kg], dst, banks[kg][:].rearrange("p (j u n) -> p j n u", j=2, u=2))
            tick()

        tanhs = {}
        es = {}

        def M(op, g, dt):
            need(("c", op, g))
            ps = bank()
            for kg in range(2):
                nc.tensor.matmul_mx(
                    out=ps[:],
                    lhsT=v_codes[:, kg, P * dt : P * (dt + 1)].bitcast(X4),
                    lhsT_scale=v_sc[:, kg, P * dt : P * (dt + 1)],
                    rhs=codes[op, g][:, kg, :].bitcast(X4),
                    rhs_scale=scales[op, g][:, kg, :],
                    start=(kg == 0),
                    stop=(kg == 1),
                )

            def tanh():
                th = work.tile([P, 512], F32, name="th_" + op, tag="th_" + op, bufs=(9 if op == "t" else 4), align_bytes=64)
                if op == "h" and ACC(g, dt):
                    nc.scalar.activation(th[:], ps[:], ACT.Tanh, bias=nb_col[:, dt : dt + 1], scale=-1.0)
                else:
                    nc.scalar.activation(th[:], ps[:], ACT.Tanh, bias=b_col[:, dt : dt + 1])
                tanhs[op, g, dt] = th

            def sub():
                e = work.tile([P, 512], F32, name="e", tag="e", bufs=3, align_bytes=64)
                nc.vector.tensor_tensor(out=e[:], in0=tanhs["t", g, dt][:], in1=tanhs["h", g, dt][:], op=ALU.subtract)
                es[g, dt] = e

            later(LM, ("e", g, dt), tanh)
            if op == "h" and not ACC(g, dt):
                later(LS, ("e", g, dt), sub)
            tick()

        qb = {}

        def E(g, dt):
            need(("e", g, dt))
            ps = bank()
            for j in range(4):
                js = slice(P * j, P * (j + 1))
                if ACC(g, dt):
                    for op in "th":
                        nc.tensor.matmul(
                            ps[:, js], tanhs[op, g, dt][:, js], ident[:], start=(op == "t"), stop=(op == "h"), is_transpose=True
                        )
                else:
                    nc.tensor.transpose(ps[:, js], es[g, dt][:, js], ident[:])

            def mul():
                need(("s", g, dt // 4))
                if dt % 4 == 0:
                    qb[g, dt // 4] = work.tile([P, 512, 4], BF16, name="qb", tag="qb", bufs=2, align_bytes=64)
                nc.vector.tensor_tensor(
                    out=qb[g, dt // 4][:, P * (dt % 4) : P * (dt % 4 + 1), :],
                    in0=ps[:].rearrange("p (j d) -> p d j", j=4),
                    in1=csig[g][:, :, P * dt : P * (dt + 1)].rearrange("p j d -> p d j"),
                    op=ALU.mult,
                )

            def quant():
                cols = slice(512 * (dt // 4), 512 * (dt // 4 + 1))
                nc.vector.quantize_mx(
                    out=q_codes[:, g, cols].bitcast(X4),
                    scales=q_sc[:, g, cols],
                    in_=qb[g, dt // 4][:].rearrange("p d j -> p (d j)"),
                )

            later(LE, ("q", g, dt // 4), mul)
            if dt % 4 == 3:
                later(LEQ, ("q", g, dt // 4), quant)
            tick()

        def SIG(g, k, CENG="V"):
            cols = slice(512 * k, 512 * (k + 1))
            nc.scalar.activation(csig[g][:, :, cols], raw["a", g][:, :, cols], ACT.Sigmoid)

            def cmul():
                for j in range(4):
                    s = csig[g][:, j, cols]
                    if CENG == "V":
                        nc.vector.tensor_scalar(out=s, in0=s, scalar1=c_col[:, g, j : j + 1], scalar2=None, op0=ALU.mult)
                    else:
                        nc.gpsimd.tensor_scalar(
                            out=s, in0=s, scalar1=c_col[:, g, j : j + 1], scalar2=0.0, op0=ALU.mult, op1=ALU.add
                        )

            later(LC, ("s", g, k), cmul)

        def X(g, half, XENG="V"):
            xg = work.tile([P, 512, 4], BF16, name="xg", tag="xg", bufs=2, align_bytes=64)
            cols = slice(512 * half, 512 * (half + 1))
            dst = xg[:]
            srcx = raw["x", g][:, :, cols].rearrange("p j e -> p e j")
            if XENG == "V":
                nc.vector.tensor_copy(out=dst, in_=srcx)
            elif XENG == "A":
                nc.scalar.copy(out=dst, in_=srcx)
            else:
                for i in range(4):
                    cc = slice(512 * half + 128 * i, 512 * half + 128 * (i + 1))
                    nc.gpsimd.tensor_scalar(
                        out=xg[:, 128 * i : 128 * (i + 1), :],
                        in0=raw["x", g][:, :, cc].rearrange("p j e -> p e j"),
                        scalar1=1.0, scalar2=0.0, op0=ALU.mult, op1=ALU.add,
                    )

            def quant():
                nc.vector.quantize_mx(
                    out=x_codes[:, g, cols].bitcast(X4), scales=x_sc[:, g, cols], in_=xg[:].rearrange("p e j -> p (e j)")
                )

            later(LX, ("x", g), quant)

        ufs = {}
        ub = {}

        def unit(G, et):
            return (et, 1) if G == 1 and et >= 6 else (et - et % 2, 2)

        def S2(G, et, eng):
            for g in range(2):
                need(("x", g))
                need(("q", g, G))
            ps = bank()
            for g in range(2):
                nc.tensor.matmul_mx(
                    out=ps[:],
                    lhsT=x_codes[:, g, P * et : P * (et + 1)].bitcast(X4),
                    lhsT_scale=x_sc[:, g, P * et : P * (et + 1)],
                    rhs=q_codes[:, g, 512 * G : 512 * (G + 1)].bitcast(X4),
                    rhs_scale=q_sc[:, g, 512 * G : 512 * (G + 1)],
                    start=(g == 0),
                    stop=(g == 1),
                )
            e0, n = unit(G, et)
            if et == e0:
                ufs[G, e0] = work.tile([P, 2, 512], F32, name="uf", tag="uf", bufs=4, align_bytes=64)
                ub[G, e0] = work.tile([P, 1024], BF16, name="u16", tag="u16", bufs=4, align_bytes=64)
            uf = ufs[G, e0]
            u16 = ub[G, e0]
            i = et - e0

            def evac():
                if eng == "A":
                    nc.scalar.activation(uf[:, i, :], ps[:], ACT.Copy, scale=1.0 / 32.0)
                else:
                    nc.vector.tensor_scalar(out=uf[:, i, :], in0=ps[:], scalar1=1.0 / 32.0, scalar2=None, op0=ALU.mult)

            def cast():
                nc.vector.tensor_copy(
                    out=u16[:, 0 : 512 * n].rearrange("e (u w i) -> e u w i", u=2, i=2),
                    in_=uf[:, 0:n, :].rearrange("e k (w u i) -> e u (k w) i", u=2, i=2),
                )
                nc.sync.dma_start(
                    out=out_0[P * e0 : P * (e0 + n), 512 * G : 512 * (G + 1)].rearrange("(k e) d -> e k d", k=n),
                    in_=uf[:, 0:n, :],
                )

            later(LU, ("u", G, e0), evac)
            if i == n - 1:
                later(LUC, ("u", G, e0), cast)
            tick()

        def U(G, e0, eng):
            need(("u", G, e0))
            n = unit(G, e0)[1]
            ps = bank()
            words = ub[G, e0][:, 0 : 512 * n].bitcast(F32)
            for i in range(n):
                for u in range(2):
                    o = 256 * i + 128 * u
                    w = 128 * n * u + 128 * i
                    nc.tensor.transpose(ps[:, o : o + 128], words[:, w : w + 128], ident[:])
            pg = work.tile([P, 256, 4], BF16, name="pg", tag="pg", bufs=4, align_bytes=64)
            cols = slice(P * e0, P * (e0 + n))

            def evac():
                dst = pg[:, 0 : P * n, :].bitcast(F32).rearrange("p (i e) u -> p i e u", i=n)
                pcopy(eng, dst, ps[:, 0 : 256 * n].rearrange("p (i u e) -> p i e u", i=n, u=2))

            def quant():
                nc.vector.quantize_mx(
                    out=o_codes[:, G, cols].bitcast(X4),
                    scales=o_sc[:, G, cols],
                    in_=pg[:, 0 : P * n, :].rearrange("p e j -> p (e j)"),
                )
                last = e0 + n
                if last in STORES[G]:
                    k = STORES[G].index(last)
                    cc = slice(P * (STORES[G][k - 1] if k else 0), P * last)
                    nc.sync.dma_start(
                        out=out_1[G, :, cc, :].rearrange("p m t -> p (m t)").bitcast(I32),
                        in_=o_codes[:, G, cc].bitcast(I32),
                    )
                if last == 8:
                    for q in range(4):
                        nc.sync.dma_start(
                            out=out_2[G, 4 * q : 4 * q + 4, :].bitcast(I32),
                            in_=o_sc[32 * q : 32 * q + 4, G, :].bitcast(I32),
                        )

            later(LT, ("o", G, e0), evac)
            later(LQ, ("o", G, e0), quant)
            tick()

        FN = {"smallb": smallb, "smallc": smallc, "smallv": smallv, "T": T, "T0": T0, "M": M, "E": E, "X": X, "SIG": SIG, "S2": S2, "U": U, "load": load, "loadv": loadv, "BIAS": BIAS, "tick": tick}
        for f in PROG:
            FN[f[0]](*f[1:])
        for i in range(20):
            tick()
